import numpy as np, ml_dtypes
CORES = [19,147,275,403]
N = 4
R, T, B = 8192, 2048, 128
def entries(a): return a.T.reshape(-1)
def pack(v, P): return np.ascontiguousarray(np.asarray(v, np.int32).reshape(-1, P).T)
def lists(rng, how):
    I = rng.integers(0, N * R, (N, T)); E = np.sort(rng.integers(0, T + 1, (N, B)), axis=1)
    if how == "void":
        E = np.zeros((N, B), np.int64)
        for r in range(N): k = np.sort(1 + rng.permutation(B - 2)[:6]); c = np.sort(1 + rng.permutation(T)[:6]); E[r] = np.concatenate([[0], c])[np.searchsorted(k, np.arange(B), side="right")]
        E[rng.integers(N)] = 0
    if how == "one":
        p = rng.permutation(N); z = rng.integers(0, B, N); z[p[0]] = 0; z[p[1]] = B - 1; E = np.where(np.arange(B)[None, :] < z[:, None], 0, T)
        I[p[::2]] = R * p[1] + I[p[::2]] % R
    if how == "single": E = np.broadcast_to(1 + np.arange(B), (N, B)).copy()
    if how == "hotrank": I = R * int(rng.integers(N)) + rng.integers(0, R, (N, T))
    if how == "edge": I = R * rng.integers(0, N, (N, T)) + np.where(rng.random((N, T)) < 0.5, 0, R - 1); E[:, -1] = T
    return {"idx": np.stack([pack(i, 16) for i in I]), "end": np.stack([pack(v, 16) for v in E])}
def setup_inputs(rng):
    return dict({"tab": rng.standard_normal((N, 128, R), dtype=np.float32).astype(ml_dtypes.bfloat16)}, **lists(rng, "uniform"))
def setup_inputs_edge(rng):
    d = setup_inputs(rng); d.update(lists(rng, "edge"))
    for k in ("tab",): d[k] = (d[k].astype(np.float32) * 1048576.0).astype(d[k].dtype)
    return d
def setup_inputs_hotrank(rng):
    d = setup_inputs(rng); d.update(lists(rng, "hotrank"))
    for k in ("tab",): d[k] = (d[k].astype(np.float32) * (1 / 1024.0)).astype(d[k].dtype)
    return d
def setup_inputs_one(rng):
    d = setup_inputs(rng); d.update(lists(rng, "one"))
    return d
def setup_inputs_single(rng):
    d = setup_inputs(rng); d.update(lists(rng, "single"))
    return d
def setup_inputs_void(rng):
    d = setup_inputs(rng); d.update(lists(rng, "void"))
    return d
def check_inputs(x):
    bad = []
    if x["idx"].min() < 0 or x["idx"].max() >= N * R: bad.append("idx out of range")
    if x["end"].min() < 0 or x["end"].max() >= T + 1: bad.append("end out of range")
    if any((np.diff(entries(a)) < 0).any() for a in x["end"]): bad.append("end falls")
    t = x["tab"].astype(np.float32)
    if t.min() < -1e30 or t.max() > 1e30: bad.append("tab beyond -1e30 to 1e30")
    return bad
def reference(tab, idx, end):
    A = np.concatenate(list(tab), axis=1)
    y = np.zeros((N, 128, B), tab.dtype)
    for r in range(N):
        G = A[:, entries(idx[r])]; c = np.concatenate([[0], entries(end[r])])
        for b in range(B):
            if c[b + 1] > c[b]: y[r][:, b] = G[:, c[b]:c[b + 1]].max(axis=1)
    return {"y": y}

@@ -1,0 +1,359 @@
+import numpy as np
+from concourse.bass import DstId, RemoteDMATransfer
+from concourse.mybir import dt, AluOpType, AxisListType, ActivationFunctionType
+
+M = 9.953037915854457e+29
+COLS = 8192
+PAD = 8
+LEN = 2048
+TABS = [6144, 2048]
+GATE = 1
+LISTS = "OCID"
+PS = {"O": "psA", "C": "psA", "I": "psB", "D": "psA"}
+BANK = {"O": 0, "C": 1, "I": 2}
+CONV = "OC"
+
+
+def gs(q, *cuts):
+    return [("g", q, a, b) for a, b in zip(cuts, cuts[1:])]
+
+
+def sc(q, *cuts):
+    return [("scan", q, a, b) for a, b in zip(cuts, cuts[1:])]
+
+
+T_ORDER = [("un", "O"), ("cap", "O"), ("un", "C"), ("un", "I"), ("cap", "C"), ("cap", "I"), ("cap", "D")]
+S_ORDER = ([("conv", "O", h) for h in range(4)] + gs("O", 0, 672, 1344) + [("conv", "C", h) for h in range(4)]
+           + gs("D", 0, 512, 1024, 1344) + gs("I", 0, 512, 1024, 1536, 1920) + gs("C", 0, 1024, 2048))
+V_ORDER = ([("unA", "O"), ("unB", "O"), ("flags", "O"), ("unA", "C"), ("unA", "I"), ("unB", "C"), ("flags", "C"), ("unB", "I")]
+           + gs("O", 1344, 2048) + [("flags", "I")] + sc("O", 0, 672, 1344, 2048) + [("flags", "D")] + gs("D", 1344, 2048)
+           + sc("D", 0, 512, 1024, 1536, 2048) + [("pick", "D")] + gs("I", 1920, 2048) + sc("I", 0, 512, 1024, 1536, 2048)
+           + [("pick", "I")] + sc("C", 0, 1024, 2048) + [("pick", "C"), ("acc", "O"), ("fin", "O")])
+G_SENDS = ["D", "I", "C"]
+
+SCRATCH = {
+    "win": ("sbuf", [128, COLS + 2 * PAD], "bfloat16"),
+    "pcol": ("sbuf", [128, 8], "int32"),
+    "pmod": ("sbuf", [128, 8], "int32"),
+    "rep": ("sbuf", [128, 8], "uint16"),
+    "mki": ("sbuf", [128, 136], "int32"),
+    "MK": ("sbuf", [128, 136], "float32"),
+    "seli": ("sbuf", [128, 128], "int32"),
+    "SEL": ("sbuf", [128, 128], "float32"),
+    "cc": ("sbuf", [128, 8], "bfloat16"),
+    "hl": ("sbuf", [128, 8], "bfloat16"),
+    "hilo": ("sbuf", [128, 8], "int32"),
+    "ef": ("sbuf", [128, 8], "float32"),
+    "IH": ("sbuf", [128, 512], "bfloat16"),
+    "IL": ("sbuf", [128, 512], "bfloat16"),
+    "LD": ("sbuf", [128, 128], "bfloat16"),
+    "LC": ("sbuf", [128, 128], "bfloat16"),
+    "LI": ("sbuf", [128, 128], "bfloat16"),
+    "acc": ("sbuf", [128, 128], "bfloat16"),
+    "Y": ("sbuf", [128, 128], "bfloat16"),
+    "psA": ("psum", [128, 2048], "float32"),
+    "psB": ("psum", [128, 2048], "float32"),
+}
+SEMAPHORES = ["d_idx", "d_end", "d_tab", "d_y", "gate", "m_x", "m_win", "m_ih", "i_p", "i_mk", "i_sel", "i_il", "v_rep", "v_mka",
+              "v_MK", "v_sela", "v_SEL", "v_pm", "v_c", "v_cn", "v_il1", "v_il2", "v_ih", "v_il", "loc", "r_LD", "r_LC", "r_LI",
+              "v_acc", "v_Y", "v_pku", "v_pkh"]
+for _q in LISTS:
+    SCRATCH["off" + _q] = ("sbuf", [128, 128], "uint16")
+    SCRATCH["LH" + _q] = ("sbuf", [128, 512], "bfloat16")
+    SCRATCH["RL" + _q] = ("sbuf", [128, 512], "bfloat16")
+    SCRATCH["G" + _q] = ("sbuf", [128, LEN], "bfloat16")
+    SCRATCH["S" + _q] = ("sbuf", [128, LEN + 8], "bfloat16")
+    SCRATCH["pk" + _q] = ("sbuf", [128, 138], "uint16")
+    SEMAPHORES += ["m_s" + _q, "off" + _q, "hl" + _q, "lr" + _q]
+    SEMAPHORES += ["ps%s%d" % (_q, _h) for _h in range(4)]
+    if _q in CONV:
+        SCRATCH["F" + _q] = ("sbuf", [128, LEN], "bfloat16")
+        SEMAPHORES += ["f%s%d" % (_q, _h) for _h in range(4)]
+    if _q != "D":
+        SCRATCH["X" + _q] = ("sbuf", [128, 18], "int32")
+        SCRATCH["Z" + _q] = ("sbuf", [128, 136], "float32")
+        SEMAPHORES += ["ef" + _q, "Z" + _q, "un" + _q, "hi" + _q] + (["pk" + _q] if _q != "C" else [])
+    if _q != "O":
+        SCRATCH["P" + _q] = ("sbuf", [128, 128], "bfloat16")
+        SEMAPHORES += ["r_" + _q, "v_P" + _q]
+SEMAPHORES += ["g%s%d" % (_s[1], _s[2]) for _s in S_ORDER + V_ORDER if _s[0] == "g"]
+SEMAPHORES += ["s%s%d" % (_s[1], _s[2]) for _s in V_ORDER if _s[0] == "scan"]
+
+
+def rank_program(g, core, T, topo):
+    rank = T.rank_of(core)
+    if rank is None:
+        return
+    op, fn, sem = AluOpType, ActivationFunctionType, T.sem
+    v, s, t, y = g.vector, g.scalar, g.tensor, g.sync
+
+    near = [k for k in T.cores if k != core and topo.may_write(core, k)]
+    i = [k for k in near if topo.rack(topo.host(k)) == topo.rack(topo.host(core))][0]
+    c = [k for k in near if k != i][0]
+    mi, mc = topo.mask(core, i), topo.mask(core, c)
+    ni, nc = bin(mi).count("1"), bin(mc).count("1")
+
+    def send(dst, mask, out, src, rsem):
+        rid, pid = topo.addr(dst, core)
+        g.remote_dma(out_ap=out, in_ap=src, remote_sem=rsem, local_sem=sem.loc, pid=pid, routing_id=rid, dma_engine_mask=mask)
+
+    arrive = {"I": ni, "D": ni, "C": nc}
+    base = rank * COLS
+
+    y.dma_start(T.XO[:, 0:16], T.idx[:]).then_inc(sem.d_idx, 16)
+    y.wait_ge(sem.m_x, 1)
+    y.dma_start(T.XO[1:8, 17:18], T.end[15:16, 0:7]).then_inc(sem.d_end, 16)
+    s.wait_ge(sem.m_x, 1)
+    s.dma_start(T.XO[:, 16:17], T.end[:]).then_inc(sem.d_end, 16)
+    s.dma_start(T.XO[8:128, 17:18], T.end[0:15, :]).then_inc(sem.d_end, 16)
+    a = 0
+    for n, w in enumerate(TABS):
+        e = s
+        if GATE and n >= GATE:
+            e = y
+            if n == GATE:
+                y.wait_ge(sem.gate, 1)
+        e.dma_start(T.win[:, PAD + a:PAD + a + w], T.tab[:, a:a + w]).then_inc(sem.d_tab, 16)
+        a += w
+
+    g.iota(T.pcol[:], [[0, 8]], 0, 1).then_inc(sem.i_p, 1)
+    g.iota(T.mki[:, 0:128], [[-1, 8], [0, 16]], 0, 1).then_inc(sem.i_mk, 1)
+    g.iota(T.mki[:, 128:136], [[-1, 8]], 0, 1).then_inc(sem.i_mk, 1)
+    g.iota(T.seli[:], [[0, 8], [-8, 16]], 0, 1).then_inc(sem.i_sel, 1)
+    g.iota(T.IL[:, 0:128], [[1, 128]], -256, 0, allow_small_or_imprecise_dtypes=True).then_inc(sem.i_il, 1)
+
+    cA, cB, cU, cW, cN = [T.cc[:, k:k + 1] for k in range(5)]
+    v.memset(T.XO[0:1, 16:18], 0).then_inc(sem.m_x, 1)
+    v.memset(T.win[:, 0:PAD], -M).then_inc(sem.m_win, 1)
+    v.memset(T.win[:, PAD + COLS:PAD + COLS + PAD], -M).then_inc(sem.m_win, 1)
+    v.wait_ge(sem.i_p, 1)
+    v.tensor_scalar(T.pmod[:], T.pcol[:], 15, None, op.bitwise_and).then_inc(sem.v_pm, 1)
+    v.tensor_scalar(cA, T.pcol[:, 0:1], 127.0, None, op.is_lt).then_inc(sem.v_c, 1)
+    v.tensor_scalar(cB, T.pcol[:, 0:1], 127.0, 300.0, op.is_equal, op.mult).then_inc(sem.v_c, 1)
+    v.tensor_scalar(cU, T.pcol[:, 0:1], 127.0, 556.0, op.is_equal, op.mult).then_inc(sem.v_c, 1)
+    v.tensor_scalar(cN, T.pcol[:, 0:1], 127.0, -5.0, op.is_equal, op.mult).then_inc(sem.v_cn, 1)
+    v.wait_ge(sem.v_pm, 1)
+    v.tensor_copy(T.rep[:], T.pmod[:]).then_inc(sem.v_rep, 1)
+    v.wait_ge(sem.v_cn, 1)
+    v.tensor_scalar(cW, cN, 4.0, None, op.add).then_inc(sem.v_c, 1)
+    v.wait_ge(sem.i_mk, 2)
+    v.tensor_scalar(T.mki[:], T.mki[:], 7, None, op.bitwise_and).then_inc(sem.v_mka, 1)
+    v.wait_ge(sem.i_sel, 1)
+    v.tensor_scalar(T.seli[:], T.seli[:], 3, None, op.arith_shift_right).then_inc(sem.v_sela, 1)
+    v.wait_ge(sem.v_mka, 1)
+    v.tensor_scalar(T.MK[:], T.mki[:], 0.0, None, op.is_equal).then_inc(sem.v_MK, 1)
+    v.wait_ge(sem.v_sela, 1)
+    v.tensor_scalar(T.SEL[:], T.seli[:], 0.0, None, op.is_equal).then_inc(sem.v_SEL, 1)
+    for h in range(4):
+        v.memset(T.IH[:, 128 * h:128 * h + 128], float(h - 256)).then_inc(sem.m_ih, 1)
+    v.wait_ge(sem.i_il, 1)
+    v.tensor_scalar(T.IL[:, 128:256], T.IL[:, 0:128], 128.0, None, op.add).then_inc(sem.v_il1, 1)
+    for q in LISTS:
+        v.memset(T["S" + q][:, 0:1], 0.0).then_inc(sem["m_s" + q], 1)
+    v.wait_ge(sem.v_il1, 1)
+    v.tensor_scalar(T.IL[:, 256:512], T.IL[:, 0:256], 256.0, None, op.add).then_inc(sem.v_il2, 1)
+    v.wait_ge(sem.m_ih, 4)
+    v.wait_ge(sem.v_c, 4)
+    v.tensor_scalar(T.IH[:], T.IH[:], cA, cB, op.mult, op.add).then_inc(sem.v_ih, 1)
+    v.wait_ge(sem.v_il2, 1)
+    v.tensor_scalar(T.IL[:], T.IL[:], cA, cB, op.mult, op.add).then_inc(sem.v_il, 1)
+
+    for name, n in (("d_idx", 16), ("d_end", 48), ("m_x", 1)):
+        g.wait_ge(sem[name], n)
+    send(c, mc, T.XC[:], T.XO[:], sem.r_C)
+    if GATE:
+        g.sem_inc(sem.gate, 1)
+    send(i, mi, T.XI[:], T.XO[:], sem.r_I)
+    g.wait_ge(sem.v_pku, 1)
+    g.wait_ge(sem.v_pkh, 1)
+    send(i, mi, T.pkD[:], T.pkC[:], sem.r_D)
+
+    scans = {}
+    for st in V_ORDER:
+        if st[0] == "scan":
+            scans.setdefault(st[1], []).append((st[2], st[3]))
+    gathers = {}
+    for st in S_ORDER + V_ORDER:
+        if st[0] == "g":
+            gathers.setdefault(st[1], []).append((st[2], st[3]))
+
+    held = {}
+    first_un = [True]
+    for what, q in T_ORDER:
+        if what == "un":
+            if first_un[0]:
+                t.wait_ge(sem.v_SEL, 1)
+                first_un[0] = False
+            t.wait_ge(sem["Z" + q], 2)
+            k = 512 * BANK[q]
+            t.matmul(T.psB[:, k:k + 136], T.SEL[:], T["Z" + q][:], True, True).then_inc(sem["un" + q], 1)
+            continue
+        ps, was = T[PS[q]], held.get(PS[q])
+        held[PS[q]] = q
+        t.wait_ge(sem["lr" + q], 2)
+        for h in range(4):
+            if PS[q] == "psB" and was is None:
+                for q2 in BANK:
+                    if BANK[q2] == h:
+                        t.wait_ge(sem["off" + q2], 1)
+                        if q2 == "C":
+                            t.wait_ge(sem.v_pku, 1)
+                        else:
+                            t.wait_ge(sem["pk" + q2], 2)
+            if was is not None and was in CONV:
+                t.wait_ge(sem["f%s%d" % (was, h)], 1)
+            elif was is not None:
+                for a, b in scans[was]:
+                    if a < 512 * h + 512 and b > 512 * h:
+                        t.wait_ge(sem["s%s%d" % (was, a)], 1)
+            t.matmul(ps[:, 512 * h:512 * h + 512], T["LH" + q][:, 128 * h:128 * h + 128], T["RL" + q][:], True,
+                     True).then_inc(sem["ps%s%d" % (q, h)], 1)
+
+    waited = {}
+
+    def wait(e, eng, name, n):
+        if (eng, name) not in waited:
+            waited[eng, name] = 1
+            e.wait_ge(sem[name], n)
+
+    def two(t2, q):
+        k = 2 * LISTS.index(q)
+        return t2[:, k:k + 1], t2[:, k + 1:k + 2], t2[:, k:k + 2]
+
+    def unA(q):
+        X = T["X" + q]
+        end, ne, _ = two(T.ef, q)
+        hi, lo, hilo = two(T.hilo, q)
+        if q in arrive:
+            wait(v, "v", "r_" + q, arrive[q])
+        else:
+            wait(v, "v", "d_idx", 16)
+            wait(v, "v", "d_end", 48)
+            wait(v, "v", "m_x", 1)
+        wait(v, "v", "v_rep", 1)
+        wait(v, "v", "v_MK", 1)
+        v.tensor_copy(end, X[:, 16:17]).then_inc(sem["ef" + q], 1)
+        v.tensor_tensor(ne, X[:, 16:17], X[:, 17:18], op.not_equal).then_inc(sem["ef" + q], 1)
+        v.tensor_tensor(T["Z" + q][:, 0:128], X[:, 0:16].indirect(T.rep[:]), T.MK[:, 0:128], op.mult).then_inc(sem["Z" + q], 1)
+        wait(v, "v", "ef" + q, 2)
+        v.tensor_scalar(T["Z" + q][:, 128:136], T.MK[:, 128:136], end, ne, op.mult, op.mult).then_inc(sem["Z" + q], 1)
+        v.tensor_scalar(hi, X[:, 16:17], 9, None, op.arith_shift_right).then_inc(sem["hi" + q], 1)
+        v.tensor_scalar(lo, X[:, 16:17], 511, None, op.bitwise_and).then_inc(sem["hi" + q], 1)
+        wait(v, "v", "hi" + q, 2)
+        wait(v, "v", "v_c", 4)
+        name = "v_pkh" if q == "C" else "pk" + q
+        v.tensor_scalar(T["pk" + q][:, 136:138], hilo, cA, cU, op.mult, op.add).then_inc(sem[name], 1)
+
+    def unB(q):
+        k = 512 * BANK[q]
+        ps, pk = T.psB, T["pk" + q]
+        wait(v, "v", "un" + q, 1)
+        if q == "C":
+            v.tensor_copy(pk[:, 0:136], ps[:, k:k + 136]).then_inc(sem.v_pku, 1)
+        v.tensor_scalar(T["off" + q][:], ps[:, k:k + 128], float(PAD - base), float(PAD + COLS), op.add, op.min
+                        ).then_inc(sem["off" + q], 1)
+        if q != "C":
+            v.tensor_copy(pk[:, 128:136], ps[:, k + 128:k + 136]).then_inc(sem["pk" + q], 1)
+
+    def flags(q):
+        pk = T["pk" + q]
+        hi, lo, hilo = two(T.hl, q)
+        if q == "D":
+            wait(v, "v", "r_D", ni)
+            v.tensor_scalar(T.offD[:], pk[:, 0:128], float(PAD - base), float(PAD + COLS), op.add, op.min).then_inc(sem.offD, 1)
+        elif q == "C":
+            wait(v, "v", "v_pkh", 1)
+        else:
+            wait(v, "v", "pk" + q, 2)
+        v.tensor_scalar(hilo, pk[:, 136:138], -256.0, None, op.add).then_inc(sem["hl" + q], 1)
+        wait(v, "v", "v_ih", 1)
+        wait(v, "v", "v_il", 1)
+        v.wait_ge(sem["hl" + q], 1)
+        v.tensor_scalar(T["LH" + q][:], T.IH[:], hi, -M, op.is_equal, op.mult).then_inc(sem["lr" + q], 1)
+        v.tensor_scalar(T["RL" + q][:], T.IL[:], lo, cW, op.is_equal, op.mult).then_inc(sem["lr" + q], 1)
+
+    def conv(e, eng, q, h):
+        wait(e, eng, "ps%s%d" % (q, h), 1)
+        out, src = T["F" + q][:, 512 * h:512 * h + 512], T[PS[q]][:, 512 * h:512 * h + 512]
+        ins = s.activation(out, src, fn.Copy) if eng == "s" else v.tensor_copy(out, src)
+        ins.then_inc(sem["f%s%d" % (q, h)], 1)
+
+    def gath(e, eng, q, a, b):
+        wait(e, eng, "d_tab", 16 * len(TABS))
+        wait(e, eng, "m_win", 2)
+        wait(e, eng, "off" + q, 1)
+        src, out = T.win[:].indirect(T["off" + q][:, a // 16:b // 16]), T["G" + q][:, a:b]
+        ins = s.activation(out, src, fn.Copy) if eng == "s" else v.tensor_copy(out, src)
+        ins.then_inc(sem["g%s%d" % (q, a)], 1)
+
+    def scan(q, a, b):
+        S = T["S" + q]
+        for a2, b2 in gathers[q]:
+            if a2 < b and b2 > a:
+                wait(v, "v", "g%s%d" % (q, a2), 1)
+        for h in range(a // 512, (b + 511) // 512):
+            wait(v, "v", "%s%s%d" % ("f" if q in CONV else "ps", q, h), 1)
+        for a2, b2 in scans[q]:
+            if b2 == a:
+                wait(v, "v", "s%s%d" % (q, a2), 1)
+        cap = T["F" + q] if q in CONV else T[PS[q]]
+        v.tensor_tensor_scan(S[:, a + 1:b + 1], cap[:, a:b], T["G" + q][:, a:b], -M if a == 0 else S[:, a:a + 1], op.min, op.max
+                             ).then_inc(sem["s%s%d" % (q, a)], 1)
+
+    def picks(q):
+        wait(v, "v", "s%s%d" % (q, scans[q][-1][0]), 1)
+        wait(v, "v", "m_s" + q, 1)
+        if q == "C":
+            wait(v, "v", "v_pku", 1)
+        elif q != "D":
+            wait(v, "v", "pk" + q, 2)
+        return T["S" + q][:, 0:LEN + 1].indirect(T["pk" + q][:, 128:136])
+
+    for st in V_ORDER:
+        what, q = st[0], st[1]
+        if what == "unA":
+            unA(q)
+        elif what == "unB":
+            unB(q)
+        elif what == "flags":
+            flags(q)
+        elif what == "conv":
+            conv(v, "v", q, st[2])
+        elif what == "g":
+            gath(v, "v", q, st[2], st[3])
+        elif what == "scan":
+            scan(q, st[2], st[3])
+        elif what == "pick":
+            src = picks(q)
+            v.tensor_copy(T["P" + q][:], src).then_inc(sem["v_P" + q], 1)
+        elif what == "acc":
+            src = picks(q)
+            v.wait_ge(sem.r_LI, ni)
+            v.tensor_tensor(T.acc[:], src, T.LI[:], op.max).then_inc(sem.v_acc, 1)
+        else:
+            v.wait_ge(sem.v_acc, 1)
+            v.wait_ge(sem.r_LC, nc)
+            v.tensor_tensor(T.Y[:], T.acc[:], T.LC[:], op.max).then_inc(sem.v_Y, 1)
+
+    for st in S_ORDER:
+        if st[0] == "conv":
+            conv(s, "s", st[1], st[2])
+        else:
+            gath(s, "s", st[1], st[2], st[3])
+
+    for q in G_SENDS:
+        g.wait_ge(sem["v_P" + q], 1)
+        if q == "D":
+            send(i, mi, T.LD[:], T.PD[:], sem.r_LD)
+        elif q == "I":
+            send(i, mi, T.LI[:], T.PI[:], sem.r_LI)
+        else:
+            g.wait_ge(sem.r_LD, ni)
+            rid, pid = topo.addr(c, core)
+            g.remote_dma_fused([RemoteDMATransfer(dst_ids=[DstId(rid=rid, pnc=pid)], dma_engine_mask=mc, remote_sem=sem.r_LC,
+                                                  srcs=[T.PC[:], T.LD[:]], dsts=[T.LC[:]], alu_op=2)], local_sem=sem.loc)
+    g.wait_ge(sem.loc, 4 * ni + 2 * nc)
+
+    y.wait_ge(sem.v_Y, 1)
+    y.dma_start(T.y[:], T.Y[:]).then_inc(sem.d_y, 16)
+    y.wait_ge(sem.d_y, 16)

@@ -8,10 +8,8 @@ PAD = 8
 LEN = 2048
 TABS = [6144, 2048]
 GATE = 1
-LISTS = "OCID"
-PS = {"O": "psA", "C": "psA", "I": "psB", "D": "psA"}
-BANK = {"O": 0, "C": 1, "I": 2}
-CONV = "OC"
+HLISTS = "OCI"
+BANK = {"O": 0, "C": 1, "I": 2, "D": 3}
 
 
 def gs(q, *cuts):
@@ -22,14 +20,14 @@ def sc(q, *cuts):
     return [("scan", q, a, b) for a, b in zip(cuts, cuts[1:])]
 
 
-T_ORDER = [("un", "O"), ("cap", "O"), ("un", "C"), ("un", "I"), ("cap", "C"), ("cap", "I"), ("cap", "D")]
-S_ORDER = ([("conv", "O", h) for h in range(4)] + gs("O", 0, 672, 1344) + [("conv", "C", h) for h in range(4)]
-           + gs("D", 0, 512, 1024, 1344) + gs("I", 0, 512, 1024, 1536, 1920) + gs("C", 0, 1024, 2048))
-V_ORDER = ([("unA", "O"), ("unB", "O"), ("flags", "O"), ("unA", "C"), ("unA", "I"), ("unB", "C"), ("flags", "C"), ("unB", "I")]
-           + gs("O", 1344, 2048) + [("flags", "I")] + sc("O", 0, 672, 1344, 2048) + [("flags", "D")] + gs("D", 1344, 2048)
-           + sc("D", 0, 512, 1024, 1536, 2048) + [("pick", "D")] + gs("I", 1920, 2048) + sc("I", 0, 512, 1024, 1536, 2048)
-           + [("pick", "I")] + sc("C", 0, 1024, 2048) + [("pick", "C"), ("acc", "O"), ("fin", "O")])
-G_SENDS = ["D", "I", "C"]
+T_ORDER = [("un", "O"), ("un", "C"), ("un", "I"), ("un", "D"), ("caps", "D")]
+S_ORDER = (gs("C", 0, 1024, 1600) + gs("D", 0, 512, 1024, 1280) + gs("I", 0, 1024, 2048) + [("pick", "I")]
+           + gs("O", 0, 1024, 2048))
+V_ORDER = ([("unA", "O"), ("unB", "O"), ("unA", "C"), ("unA", "I"), ("unB", "C"), ("unB", "I")] + gs("C", 1600, 2048)
+           + [("unA", "D"), ("flags", "D"), ("unB", "D")] + gs("D", 1280, 2048) + sc("D", 0, 512, 1024, 1536, 2048) + [("pick", "D")]
+           + sc("I", 0, 1024, 2048) + sc("C", 0, 1024, 2048) + [("pick", "C")] + sc("O", 0, 1024, 2048)
+           + [("acc", "O"), ("fin", "O")])
+G_ORDER = ["ends", "C", "I", "relay", "PD", "PI", "PC"]
 
 SCRATCH = {
     "win": ("sbuf", [128, COLS + 2 * PAD], "bfloat16"),
@@ -41,11 +39,14 @@ SCRATCH = {
     "seli": ("sbuf", [128, 128], "int32"),
     "SEL": ("sbuf", [128, 128], "float32"),
     "cc": ("sbuf", [128, 8], "bfloat16"),
-    "hl": ("sbuf", [128, 8], "bfloat16"),
-    "hilo": ("sbuf", [128, 8], "int32"),
+    "E": ("sbuf", [128, 1], "int32"),
+    "hilo": ("sbuf", [128, 2], "int32"),
+    "hl": ("sbuf", [128, 2], "bfloat16"),
     "ef": ("sbuf", [128, 8], "float32"),
     "IH": ("sbuf", [128, 512], "bfloat16"),
     "IL": ("sbuf", [128, 512], "bfloat16"),
+    "LH": ("sbuf", [128, 512], "bfloat16"),
+    "RL": ("sbuf", [128, 512], "bfloat16"),
     "LD": ("sbuf", [128, 128], "bfloat16"),
     "LC": ("sbuf", [128, 128], "bfloat16"),
     "LI": ("sbuf", [128, 128], "bfloat16"),
@@ -54,51 +55,175 @@ SCRATCH = {
     "psA": ("psum", [128, 2048], "float32"),
     "psB": ("psum", [128, 2048], "float32"),
 }
-SEMAPHORES = ["d_idx", "d_end", "d_tab", "d_y", "gate", "m_x", "m_win", "m_ih", "i_p", "i_mk", "i_sel", "i_il", "v_rep", "v_mka",
+SEMAPHORES = ["d_idx", "d_end", "d_y", "gate", "m_x", "m_win", "m_ih", "i_p", "i_mk", "i_sel", "i_il", "v_rep", "v_mka",
               "v_MK", "v_sela", "v_SEL", "v_pm", "v_c", "v_cn", "v_il1", "v_il2", "v_ih", "v_il", "loc", "r_LD", "r_LC", "r_LI",
-              "v_acc", "v_Y", "v_pku", "v_pkh"]
-for _q in LISTS:
+              "r_E", "v_acc", "v_Y", "hi", "hl", "lr"]
+SEMAPHORES += ["d_tab%d" % _k for _k in range(len(TABS))] + ["ps%d" % _k for _k in range(4)] + ["f%d" % _k for _k in range(4)]
+for _q in "OCID":
+    SCRATCH["X" + _q] = ("sbuf", [128, 18], "int32")
+    SCRATCH["Z" + _q] = ("sbuf", [128, 136], "float32")
     SCRATCH["off" + _q] = ("sbuf", [128, 128], "uint16")
-    SCRATCH["LH" + _q] = ("sbuf", [128, 512], "bfloat16")
-    SCRATCH["RL" + _q] = ("sbuf", [128, 512], "bfloat16")
+    SCRATCH["pk" + _q] = ("sbuf", [128, 8], "uint16")
     SCRATCH["G" + _q] = ("sbuf", [128, LEN], "bfloat16")
     SCRATCH["S" + _q] = ("sbuf", [128, LEN + 8], "bfloat16")
-    SCRATCH["pk" + _q] = ("sbuf", [128, 138], "uint16")
-    SEMAPHORES += ["m_s" + _q, "off" + _q, "hl" + _q, "lr" + _q]
-    SEMAPHORES += ["ps%s%d" % (_q, _h) for _h in range(4)]
-    if _q in CONV:
+    SEMAPHORES += ["m_s" + _q, "off" + _q, "pk" + _q, "ef" + _q, "Z" + _q, "un" + _q]
+    if _q in HLISTS:
         SCRATCH["F" + _q] = ("sbuf", [128, LEN], "bfloat16")
-        SEMAPHORES += ["f%s%d" % (_q, _h) for _h in range(4)]
-    if _q != "D":
-        SCRATCH["X" + _q] = ("sbuf", [128, 18], "int32")
-        SCRATCH["Z" + _q] = ("sbuf", [128, 136], "float32")
-        SEMAPHORES += ["ef" + _q, "Z" + _q, "un" + _q, "hi" + _q] + (["pk" + _q] if _q != "C" else [])
+        SEMAPHORES += ["r_F%s0" % _q, "r_F%s1" % _q]
     if _q != "O":
         SCRATCH["P" + _q] = ("sbuf", [128, 128], "bfloat16")
-        SEMAPHORES += ["r_" + _q, "v_P" + _q]
+        SEMAPHORES += ["v_P" + _q, "r_" + _q]
 SEMAPHORES += ["g%s%d" % (_s[1], _s[2]) for _s in S_ORDER + V_ORDER if _s[0] == "g"]
 SEMAPHORES += ["s%s%d" % (_s[1], _s[2]) for _s in V_ORDER if _s[0] == "scan"]
 
 
+def helpers_of(core, T, topo):
+    same = [k for k in range(core - 8, core + 9) if k >= 0 and topo.host(k) == topo.host(core) and topo.chip(k) == topo.chip(core)
+            and topo.die(k) == topo.die(core) and T.rank_of(k) is None]
+    return same[:len(HLISTS)]
+
+
+def neighbours(core, T, topo):
+    near = [k for k in T.cores if k != core and topo.may_write(core, k)]
+    i = [k for k in near if topo.rack(topo.host(k)) == topo.rack(topo.host(core))][0]
+    return i, [k for k in near if k != i][0]
+
+
+def engines(mask):
+    return [k for k in range(16) if mask >> k & 1]
+
+
+def as_mask(which):
+    return sum(1 << k for k in which)
+
+
+def ends_masks(rank, T, topo):
+    i, c = neighbours(rank, T, topo)
+    out = engines(topo.mask(rank, helpers_of(c, T, topo)[HLISTS.index("C")]))
+    own = [k for k in engines(topo.mask(rank, helpers_of(rank, T, topo)[HLISTS.index("O")])) if k not in out]
+    n = len(out) // 2
+    return {"C": as_mask(out[:n]), "I": as_mask(out[n:]), "O": as_mask(own[:n])}
+
+
+def constants(g, T, topo, full):
+    op, sem, v = AluOpType, T.sem, g.vector
+    cA, cB, cU, cW, cN, cV = [T.cc[:, k:k + 1] for k in range(6)]
+    g.iota(T.pcol[:], [[0, 8]], 0, 1).then_inc(sem.i_p, 1)
+    if full:
+        g.iota(T.mki[:, 0:128], [[-1, 8], [0, 16]], 0, 1).then_inc(sem.i_mk, 1)
+        g.iota(T.mki[:, 128:136], [[-1, 8]], 0, 1).then_inc(sem.i_mk, 1)
+        g.iota(T.seli[:], [[0, 8], [-8, 16]], 0, 1).then_inc(sem.i_sel, 1)
+    g.iota(T.IL[:, 0:128], [[1, 128]], -256, 0, allow_small_or_imprecise_dtypes=True).then_inc(sem.i_il, 1)
+    if full:
+        v.memset(T.XO[0:1, 16:18], 0).then_inc(sem.m_x, 1)
+        v.memset(T.win[:, 0:PAD], -M).then_inc(sem.m_win, 1)
+        v.memset(T.win[:, PAD + COLS:PAD + COLS + PAD], -M).then_inc(sem.m_win, 1)
+    v.wait_ge(sem.i_p, 1)
+    if full:
+        v.tensor_scalar(T.pmod[:], T.pcol[:], 15, None, op.bitwise_and).then_inc(sem.v_pm, 1)
+    v.tensor_scalar(cN, T.pcol[:, 0:1], 127.0, -5.0, op.is_equal, op.mult).then_inc(sem.v_cn, 1)
+    v.tensor_scalar(cV, T.pcol[:, 0:1], 127.0, -556.0, op.is_lt, op.mult).then_inc(sem.v_cn, 1)
+    v.tensor_scalar(cA, T.pcol[:, 0:1], 127.0, None, op.is_lt).then_inc(sem.v_c, 1)
+    v.tensor_scalar(cB, T.pcol[:, 0:1], 127.0, 300.0, op.is_equal, op.mult).then_inc(sem.v_c, 1)
+    if full:
+        v.wait_ge(sem.v_pm, 1)
+        v.tensor_copy(T.rep[:], T.pmod[:]).then_inc(sem.v_rep, 1)
+    v.wait_ge(sem.v_cn, 2)
+    v.tensor_scalar(cU, cV, 300.0, None, op.add).then_inc(sem.v_c, 1)
+    v.tensor_scalar(cW, cN, 4.0, None, op.add).then_inc(sem.v_c, 1)
+    if full:
+        v.wait_ge(sem.i_mk, 2)
+        v.tensor_scalar(T.mki[:], T.mki[:], 7, None, op.bitwise_and).then_inc(sem.v_mka, 1)
+        v.wait_ge(sem.i_sel, 1)
+        v.tensor_scalar(T.seli[:], T.seli[:], 3, None, op.arith_shift_right).then_inc(sem.v_sela, 1)
+        v.wait_ge(sem.v_mka, 1)
+        v.tensor_scalar(T.MK[:], T.mki[:], 0.0, None, op.is_equal).then_inc(sem.v_MK, 1)
+        v.wait_ge(sem.v_sela, 1)
+        v.tensor_scalar(T.SEL[:], T.seli[:], 0.0, None, op.is_equal).then_inc(sem.v_SEL, 1)
+    for h in range(4):
+        v.memset(T.IH[:, 128 * h:128 * h + 128], float(h - 256)).then_inc(sem.m_ih, 1)
+    v.wait_ge(sem.i_il, 1)
+    v.tensor_scalar(T.IL[:, 128:256], T.IL[:, 0:128], 128.0, None, op.add).then_inc(sem.v_il1, 1)
+    if full:
+        for q in "OCID":
+            v.memset(T["S" + q][:, 0:1], 0.0).then_inc(sem["m_s" + q], 1)
+    v.wait_ge(sem.v_il1, 1)
+    v.tensor_scalar(T.IL[:, 256:512], T.IL[:, 0:256], 256.0, None, op.add).then_inc(sem.v_il2, 1)
+    v.wait_ge(sem.m_ih, 4)
+    v.wait_ge(sem.v_c, 4)
+    v.tensor_scalar(T.IH[:], T.IH[:], cA, cB, op.mult, op.add).then_inc(sem.v_ih, 1)
+    v.wait_ge(sem.v_il2, 1)
+    v.tensor_scalar(T.IL[:], T.IL[:], cA, cB, op.mult, op.add).then_inc(sem.v_il, 1)
+
+
+def factors(v, T, end):
+    op, sem = AluOpType, T.sem
+    v.tensor_scalar(T.hilo[:, 0:1], end, 9, None, op.arith_shift_right).then_inc(sem.hi, 1)
+    v.tensor_scalar(T.hilo[:, 1:2], end, 511, None, op.bitwise_and).then_inc(sem.hi, 1)
+    v.wait_ge(sem.hi, 2)
+    v.wait_ge(sem.v_c, 4)
+    v.tensor_scalar(T.hl[:], T.hilo[:], T.cc[:, 0:1], T.cc[:, 2:3], op.mult, op.add).then_inc(sem.hl, 1)
+    v.wait_ge(sem.v_ih, 1)
+    v.wait_ge(sem.v_il, 1)
+    v.wait_ge(sem.hl, 1)
+    v.tensor_scalar(T.LH[:], T.IH[:], T.hl[:, 0:1], -M, op.is_equal, op.mult).then_inc(sem.lr, 1)
+    v.tensor_scalar(T.RL[:], T.IL[:], T.hl[:, 1:2], T.cc[:, 3:4], op.is_equal, op.mult).then_inc(sem.lr, 1)
+
+
+def caps(t, T):
+    t.wait_ge(T.sem.lr, 2)
+    for h in range(4):
+        t.matmul(T.psA[:, 512 * h:512 * h + 512], T.LH[:, 128 * h:128 * h + 128], T.RL[:], True, True
+                 ).then_inc(T.sem["ps%d" % h], 1)
+
+
+def helper_program(g, core, main, q, T, topo):
+    sem, v, s = T.sem, g.vector, g.scalar
+    i, c = neighbours(main, T, topo)
+    owner = {"O": main, "C": c, "I": i}[q]
+    constants(g, T, topo, False)
+    v.wait_ge(sem.r_E, len(engines(ends_masks(owner, T, topo)[q])))
+    factors(v, T, T.E[:])
+    caps(g.tensor, T)
+    F = T["F" + q]
+    for h in range(4):
+        e = v if h % 2 else s
+        e.wait_ge(sem["ps%d" % h], 1)
+        out, src = F[:, 512 * h:512 * h + 512], T.psA[:, 512 * h:512 * h + 512]
+        (s.activation(out, src, ActivationFunctionType.Copy) if e is s else v.tensor_copy(out, src)).then_inc(sem["f%d" % h], 1)
+    mask = topo.mask(core, main)
+    rid, pid = topo.addr(main, core)
+    for k in range(2):
+        g.wait_ge(sem["f%d" % (2 * k)], 1)
+        g.wait_ge(sem["f%d" % (2 * k + 1)], 1)
+        part = F[:, 1024 * k:1024 * k + 1024]
+        g.remote_dma(out_ap=part, in_ap=part, remote_sem=sem["r_F%s%d" % (q, k)], local_sem=sem.loc, pid=pid, routing_id=rid,
+                     dma_engine_mask=mask)
+    g.wait_ge(sem.loc, 2 * len(engines(mask)))
+
+
 def rank_program(g, core, T, topo):
-    rank = T.rank_of(core)
-    if rank is None:
+    for r in T.cores:
+        hs = helpers_of(r, T, topo)
+        if core in hs:
+            helper_program(g, core, r, HLISTS[hs.index(core)], T, topo)
+    if T.rank_of(core) is None:
         return
     op, fn, sem = AluOpType, ActivationFunctionType, T.sem
     v, s, t, y = g.vector, g.scalar, g.tensor, g.sync
-
-    near = [k for k in T.cores if k != core and topo.may_write(core, k)]
-    i = [k for k in near if topo.rack(topo.host(k)) == topo.rack(topo.host(core))][0]
-    c = [k for k in near if k != i][0]
+    base = T.rank_of(core) * COLS
+    i, c = neighbours(core, T, topo)
     mi, mc = topo.mask(core, i), topo.mask(core, c)
-    ni, nc = bin(mi).count("1"), bin(mc).count("1")
+    ni, nc = len(engines(mi)), len(engines(mc))
+    helpers = helpers_of(core, T, topo)
+    nf = {q: len(engines(topo.mask(h, core))) for q, h in zip(HLISTS, helpers)}
+    arrive = {"C": nc, "I": ni, "D": ni}
+    sent = []
 
     def send(dst, mask, out, src, rsem):
         rid, pid = topo.addr(dst, core)
         g.remote_dma(out_ap=out, in_ap=src, remote_sem=rsem, local_sem=sem.loc, pid=pid, routing_id=rid, dma_engine_mask=mask)
-
-    arrive = {"I": ni, "D": ni, "C": nc}
-    base = rank * COLS
+        sent.append(len(engines(mask)))
 
     y.dma_start(T.XO[:, 0:16], T.idx[:]).then_inc(sem.d_idx, 16)
     y.wait_ge(sem.m_x, 1)
@@ -113,102 +238,26 @@ def rank_program(g, core, T, topo):
             e = y
             if n == GATE:
                 y.wait_ge(sem.gate, 1)
-        e.dma_start(T.win[:, PAD + a:PAD + a + w], T.tab[:, a:a + w]).then_inc(sem.d_tab, 16)
+        e.dma_start(T.win[:, PAD + a:PAD + a + w], T.tab[:, a:a + w]).then_inc(sem["d_tab%d" % n], 16)
         a += w
 
-    g.iota(T.pcol[:], [[0, 8]], 0, 1).then_inc(sem.i_p, 1)
-    g.iota(T.mki[:, 0:128], [[-1, 8], [0, 16]], 0, 1).then_inc(sem.i_mk, 1)
-    g.iota(T.mki[:, 128:136], [[-1, 8]], 0, 1).then_inc(sem.i_mk, 1)
-    g.iota(T.seli[:], [[0, 8], [-8, 16]], 0, 1).then_inc(sem.i_sel, 1)
-    g.iota(T.IL[:, 0:128], [[1, 128]], -256, 0, allow_small_or_imprecise_dtypes=True).then_inc(sem.i_il, 1)
+    constants(g, T, topo, True)
 
-    cA, cB, cU, cW, cN = [T.cc[:, k:k + 1] for k in range(5)]
-    v.memset(T.XO[0:1, 16:18], 0).then_inc(sem.m_x, 1)
-    v.memset(T.win[:, 0:PAD], -M).then_inc(sem.m_win, 1)
-    v.memset(T.win[:, PAD + COLS:PAD + COLS + PAD], -M).then_inc(sem.m_win, 1)
-    v.wait_ge(sem.i_p, 1)
-    v.tensor_scalar(T.pmod[:], T.pcol[:], 15, None, op.bitwise_and).then_inc(sem.v_pm, 1)
-    v.tensor_scalar(cA, T.pcol[:, 0:1], 127.0, None, op.is_lt).then_inc(sem.v_c, 1)
-    v.tensor_scalar(cB, T.pcol[:, 0:1], 127.0, 300.0, op.is_equal, op.mult).then_inc(sem.v_c, 1)
-    v.tensor_scalar(cU, T.pcol[:, 0:1], 127.0, 556.0, op.is_equal, op.mult).then_inc(sem.v_c, 1)
-    v.tensor_scalar(cN, T.pcol[:, 0:1], 127.0, -5.0, op.is_equal, op.mult).then_inc(sem.v_cn, 1)
-    v.wait_ge(sem.v_pm, 1)
-    v.tensor_copy(T.rep[:], T.pmod[:]).then_inc(sem.v_rep, 1)
-    v.wait_ge(sem.v_cn, 1)
-    v.tensor_scalar(cW, cN, 4.0, None, op.add).then_inc(sem.v_c, 1)
-    v.wait_ge(sem.i_mk, 2)
-    v.tensor_scalar(T.mki[:], T.mki[:], 7, None, op.bitwise_and).then_inc(sem.v_mka, 1)
-    v.wait_ge(sem.i_sel, 1)
-    v.tensor_scalar(T.seli[:], T.seli[:], 3, None, op.arith_shift_right).then_inc(sem.v_sela, 1)
-    v.wait_ge(sem.v_mka, 1)
-    v.tensor_scalar(T.MK[:], T.mki[:], 0.0, None, op.is_equal).then_inc(sem.v_MK, 1)
-    v.wait_ge(sem.v_sela, 1)
-    v.tensor_scalar(T.SEL[:], T.seli[:], 0.0, None, op.is_equal).then_inc(sem.v_SEL, 1)
-    for h in range(4):
-        v.memset(T.IH[:, 128 * h:128 * h + 128], float(h - 256)).then_inc(sem.m_ih, 1)
-    v.wait_ge(sem.i_il, 1)
-    v.tensor_scalar(T.IL[:, 128:256], T.IL[:, 0:128], 128.0, None, op.add).then_inc(sem.v_il1, 1)
-    for q in LISTS:
-        v.memset(T["S" + q][:, 0:1], 0.0).then_inc(sem["m_s" + q], 1)
-    v.wait_ge(sem.v_il1, 1)
-    v.tensor_scalar(T.IL[:, 256:512], T.IL[:, 0:256], 256.0, None, op.add).then_inc(sem.v_il2, 1)
-    v.wait_ge(sem.m_ih, 4)
-    v.wait_ge(sem.v_c, 4)
-    v.tensor_scalar(T.IH[:], T.IH[:], cA, cB, op.mult, op.add).then_inc(sem.v_ih, 1)
-    v.wait_ge(sem.v_il2, 1)
-    v.tensor_scalar(T.IL[:], T.IL[:], cA, cB, op.mult, op.add).then_inc(sem.v_il, 1)
-
-    for name, n in (("d_idx", 16), ("d_end", 48), ("m_x", 1)):
-        g.wait_ge(sem[name], n)
-    send(c, mc, T.XC[:], T.XO[:], sem.r_C)
-    if GATE:
-        g.sem_inc(sem.gate, 1)
-    send(i, mi, T.XI[:], T.XO[:], sem.r_I)
-    g.wait_ge(sem.v_pku, 1)
-    g.wait_ge(sem.v_pkh, 1)
-    send(i, mi, T.pkD[:], T.pkC[:], sem.r_D)
-
-    scans = {}
-    for st in V_ORDER:
-        if st[0] == "scan":
-            scans.setdefault(st[1], []).append((st[2], st[3]))
-    gathers = {}
-    for st in S_ORDER + V_ORDER:
-        if st[0] == "g":
-            gathers.setdefault(st[1], []).append((st[2], st[3]))
-
-    held = {}
-    first_un = [True]
+    t.wait_ge(sem.v_SEL, 1)
     for what, q in T_ORDER:
-        if what == "un":
-            if first_un[0]:
-                t.wait_ge(sem.v_SEL, 1)
-                first_un[0] = False
+        if what == "caps":
+            caps(t, T)
+        else:
             t.wait_ge(sem["Z" + q], 2)
             k = 512 * BANK[q]
             t.matmul(T.psB[:, k:k + 136], T.SEL[:], T["Z" + q][:], True, True).then_inc(sem["un" + q], 1)
-            continue
-        ps, was = T[PS[q]], held.get(PS[q])
-        held[PS[q]] = q
-        t.wait_ge(sem["lr" + q], 2)
-        for h in range(4):
-            if PS[q] == "psB" and was is None:
-                for q2 in BANK:
-                    if BANK[q2] == h:
-                        t.wait_ge(sem["off" + q2], 1)
-                        if q2 == "C":
-                            t.wait_ge(sem.v_pku, 1)
-                        else:
-                            t.wait_ge(sem["pk" + q2], 2)
-            if was is not None and was in CONV:
-                t.wait_ge(sem["f%s%d" % (was, h)], 1)
-            elif was is not None:
-                for a, b in scans[was]:
-                    if a < 512 * h + 512 and b > 512 * h:
-                        t.wait_ge(sem["s%s%d" % (was, a)], 1)
-            t.matmul(ps[:, 512 * h:512 * h + 512], T["LH" + q][:, 128 * h:128 * h + 128], T["RL" + q][:], True,
-                     True).then_inc(sem["ps%s%d" % (q, h)], 1)
 
+    scans, gathers = {}, {}
+    for st in S_ORDER + V_ORDER:
+        if st[0] == "scan":
+            scans.setdefault(st[1], []).append((st[2], st[3]))
+        if st[0] == "g":
+            gathers.setdefault(st[1], []).append((st[2], st[3]))
     waited = {}
 
     def wait(e, eng, name, n):
@@ -216,20 +265,18 @@ def rank_program(g, core, T, topo):
             waited[eng, name] = 1
             e.wait_ge(sem[name], n)
 
-    def two(t2, q):
-        k = 2 * LISTS.index(q)
-        return t2[:, k:k + 1], t2[:, k + 1:k + 2], t2[:, k:k + 2]
-
-    def unA(q):
-        X = T["X" + q]
-        end, ne, _ = two(T.ef, q)
-        hi, lo, hilo = two(T.hilo, q)
-        if q in arrive:
-            wait(v, "v", "r_" + q, arrive[q])
-        else:
+    def arrived(q):
+        if q == "O":
             wait(v, "v", "d_idx", 16)
             wait(v, "v", "d_end", 48)
             wait(v, "v", "m_x", 1)
+        else:
+            wait(v, "v", "r_" + q, arrive[q])
+
+    def unA(q):
+        X, k = T["X" + q], 2 * "OCID".index(q)
+        end, ne = T.ef[:, k:k + 1], T.ef[:, k + 1:k + 2]
+        arrived(q)
         wait(v, "v", "v_rep", 1)
         wait(v, "v", "v_MK", 1)
         v.tensor_copy(end, X[:, 16:17]).then_inc(sem["ef" + q], 1)
@@ -237,49 +284,17 @@ def rank_program(g, core, T, topo):
         v.tensor_tensor(T["Z" + q][:, 0:128], X[:, 0:16].indirect(T.rep[:]), T.MK[:, 0:128], op.mult).then_inc(sem["Z" + q], 1)
         wait(v, "v", "ef" + q, 2)
         v.tensor_scalar(T["Z" + q][:, 128:136], T.MK[:, 128:136], end, ne, op.mult, op.mult).then_inc(sem["Z" + q], 1)
-        v.tensor_scalar(hi, X[:, 16:17], 9, None, op.arith_shift_right).then_inc(sem["hi" + q], 1)
-        v.tensor_scalar(lo, X[:, 16:17], 511, None, op.bitwise_and).then_inc(sem["hi" + q], 1)
-        wait(v, "v", "hi" + q, 2)
-        wait(v, "v", "v_c", 4)
-        name = "v_pkh" if q == "C" else "pk" + q
-        v.tensor_scalar(T["pk" + q][:, 136:138], hilo, cA, cU, op.mult, op.add).then_inc(sem[name], 1)
 
     def unB(q):
         k = 512 * BANK[q]
-        ps, pk = T.psB, T["pk" + q]
         wait(v, "v", "un" + q, 1)
-        if q == "C":
-            v.tensor_copy(pk[:, 0:136], ps[:, k:k + 136]).then_inc(sem.v_pku, 1)
-        v.tensor_scalar(T["off" + q][:], ps[:, k:k + 128], float(PAD - base), float(PAD + COLS), op.add, op.min
+        v.tensor_scalar(T["off" + q][:], T.psB[:, k:k + 128], float(PAD - base), float(PAD + COLS), op.add, op.min
                         ).then_inc(sem["off" + q], 1)
-        if q != "C":
-            v.tensor_copy(pk[:, 128:136], ps[:, k + 128:k + 136]).then_inc(sem["pk" + q], 1)
-
-    def flags(q):
-        pk = T["pk" + q]
-        hi, lo, hilo = two(T.hl, q)
-        if q == "D":
-            wait(v, "v", "r_D", ni)
-            v.tensor_scalar(T.offD[:], pk[:, 0:128], float(PAD - base), float(PAD + COLS), op.add, op.min).then_inc(sem.offD, 1)
-        elif q == "C":
-            wait(v, "v", "v_pkh", 1)
-        else:
-            wait(v, "v", "pk" + q, 2)
-        v.tensor_scalar(hilo, pk[:, 136:138], -256.0, None, op.add).then_inc(sem["hl" + q], 1)
-        wait(v, "v", "v_ih", 1)
-        wait(v, "v", "v_il", 1)
-        v.wait_ge(sem["hl" + q], 1)
-        v.tensor_scalar(T["LH" + q][:], T.IH[:], hi, -M, op.is_equal, op.mult).then_inc(sem["lr" + q], 1)
-        v.tensor_scalar(T["RL" + q][:], T.IL[:], lo, cW, op.is_equal, op.mult).then_inc(sem["lr" + q], 1)
-
-    def conv(e, eng, q, h):
-        wait(e, eng, "ps%s%d" % (q, h), 1)
-        out, src = T["F" + q][:, 512 * h:512 * h + 512], T[PS[q]][:, 512 * h:512 * h + 512]
-        ins = s.activation(out, src, fn.Copy) if eng == "s" else v.tensor_copy(out, src)
-        ins.then_inc(sem["f%s%d" % (q, h)], 1)
+        v.tensor_copy(T["pk" + q][:], T.psB[:, k + 128:k + 136]).then_inc(sem["pk" + q], 1)
 
     def gath(e, eng, q, a, b):
-        wait(e, eng, "d_tab", 16 * len(TABS))
+        for k in range(len(TABS)):
+            wait(e, eng, "d_tab%d" % k, 16)
         wait(e, eng, "m_win", 2)
         wait(e, eng, "off" + q, 1)
         src, out = T.win[:].indirect(T["off" + q][:, a // 16:b // 16]), T["G" + q][:, a:b]
@@ -291,23 +306,24 @@ def rank_program(g, core, T, topo):
         for a2, b2 in gathers[q]:
             if a2 < b and b2 > a:
                 wait(v, "v", "g%s%d" % (q, a2), 1)
-        for h in range(a // 512, (b + 511) // 512):
-            wait(v, "v", "%s%s%d" % ("f" if q in CONV else "ps", q, h), 1)
+        if q in HLISTS:
+            for k in range(a // 1024, (b + 1023) // 1024):
+                wait(v, "v", "r_F%s%d" % (q, k), nf[q])
+        else:
+            for h in range(a // 512, (b + 511) // 512):
+                wait(v, "v", "ps%d" % h, 1)
         for a2, b2 in scans[q]:
             if b2 == a:
                 wait(v, "v", "s%s%d" % (q, a2), 1)
-        cap = T["F" + q] if q in CONV else T[PS[q]]
+        cap = T["F" + q] if q in HLISTS else T.psA
         v.tensor_tensor_scan(S[:, a + 1:b + 1], cap[:, a:b], T["G" + q][:, a:b], -M if a == 0 else S[:, a:a + 1], op.min, op.max
                              ).then_inc(sem["s%s%d" % (q, a)], 1)
 
-    def picks(q):
-        wait(v, "v", "s%s%d" % (q, scans[q][-1][0]), 1)
-        wait(v, "v", "m_s" + q, 1)
-        if q == "C":
-            wait(v, "v", "v_pku", 1)
-        elif q != "D":
-            wait(v, "v", "pk" + q, 2)
-        return T["S" + q][:, 0:LEN + 1].indirect(T["pk" + q][:, 128:136])
+    def picked(e, eng, q):
+        wait(e, eng, "s%s%d" % (q, scans[q][-1][0]), 1)
+        wait(e, eng, "m_s" + q, 1)
+        wait(e, eng, "pk" + q, 1)
+        return T["S" + q][:, 0:LEN + 1].indirect(T["pk" + q][:])
 
     for st in V_ORDER:
         what, q = st[0], st[1]
@@ -316,18 +332,16 @@ def rank_program(g, core, T, topo):
         elif what == "unB":
             unB(q)
         elif what == "flags":
-            flags(q)
-        elif what == "conv":
-            conv(v, "v", q, st[2])
+            arrived(q)
+            factors(v, T, T.XD[:, 16:17])
         elif what == "g":
             gath(v, "v", q, st[2], st[3])
         elif what == "scan":
             scan(q, st[2], st[3])
         elif what == "pick":
-            src = picks(q)
-            v.tensor_copy(T["P" + q][:], src).then_inc(sem["v_P" + q], 1)
+            v.tensor_copy(T["P" + q][:], picked(v, "v", q)).then_inc(sem["v_P" + q], 1)
         elif what == "acc":
-            src = picks(q)
+            src = picked(v, "v", q)
             v.wait_ge(sem.r_LI, ni)
             v.tensor_tensor(T.acc[:], src, T.LI[:], op.max).then_inc(sem.v_acc, 1)
         else:
@@ -336,23 +350,45 @@ def rank_program(g, core, T, topo):
             v.tensor_tensor(T.Y[:], T.acc[:], T.LC[:], op.max).then_inc(sem.v_Y, 1)
 
     for st in S_ORDER:
-        if st[0] == "conv":
-            conv(s, "s", st[1], st[2])
+        if st[0] == "pick":
+            s.activation(T["P" + st[1]][:], picked(s, "s", st[1]), fn.Copy).then_inc(sem["v_P" + st[1]], 1)
         else:
             gath(s, "s", st[1], st[2], st[3])
 
-    for q in G_SENDS:
-        g.wait_ge(sem["v_P" + q], 1)
-        if q == "D":
+    for name, n in (("d_idx", 16), ("d_end", 48), ("m_x", 1)):
+        g.wait_ge(sem[name], n)
+    for what in G_ORDER:
+        if what == "C":
+            send(c, mc, T.XC[:], T.XO[:], sem.r_C)
+            if GATE:
+                g.sem_inc(sem.gate, 1)
+        elif what == "I":
+            send(i, mi, T.XI[:], T.XO[:], sem.r_I)
+        elif what == "ends":
+            masks, calls = ends_masks(core, T, topo), []
+            for q, r in (("C", c), ("I", i), ("O", core)):
+                rid, pid = topo.addr(helpers_of(r, T, topo)[HLISTS.index(q)], core)
+                calls.append(RemoteDMATransfer(dst_ids=[DstId(rid=rid, pnc=pid)], dma_engine_mask=masks[q], remote_sem=sem.r_E,
+                                               srcs=[T.XO[:, 16:17]], dsts=[T.E[:]]))
+                sent.append(len(engines(masks[q])))
+            g.remote_dma_fused(calls, local_sem=sem.loc)
+        elif what == "relay":
+            g.wait_ge(sem.r_C, nc)
+            send(i, mi, T.XD[:], T.XC[:], sem.r_D)
+        elif what == "PD":
+            g.wait_ge(sem.v_PD, 1)
             send(i, mi, T.LD[:], T.PD[:], sem.r_LD)
-        elif q == "I":
+        elif what == "PI":
+            g.wait_ge(sem.v_PI, 1)
             send(i, mi, T.LI[:], T.PI[:], sem.r_LI)
         else:
+            g.wait_ge(sem.v_PC, 1)
             g.wait_ge(sem.r_LD, ni)
             rid, pid = topo.addr(c, core)
             g.remote_dma_fused([RemoteDMATransfer(dst_ids=[DstId(rid=rid, pnc=pid)], dma_engine_mask=mc, remote_sem=sem.r_LC,
                                                   srcs=[T.PC[:], T.LD[:]], dsts=[T.LC[:]], alu_op=2)], local_sem=sem.loc)
-    g.wait_ge(sem.loc, 4 * ni + 2 * nc)
+            sent.append(nc)
+    g.wait_ge(sem.loc, sum(sent))
 
     y.wait_ge(sem.v_Y, 1)
     y.dma_start(T.y[:], T.Y[:]).then_inc(sem.d_y, 16)

@@ -6,10 +6,11 @@ M = 9.953037915854457e+29
 COLS = 8192
 PAD = 8
 LEN = 2048
-TABS = [6144, 2048]
-GATE = 1
-HLISTS = "OCI"
-BANK = {"O": 0, "C": 1, "I": 2, "D": 3}
+TABS = [2048, 6144]
+ROLES = "CDI"
+HOME = {"O": "D", "I": "I"}
+AWAY = "CD"
+PIECES = [(0, 1024), (1024, 2048)]
 
 
 def gs(q, *cuts):
@@ -20,14 +21,11 @@ def sc(q, *cuts):
     return [("scan", q, a, b) for a, b in zip(cuts, cuts[1:])]
 
 
-T_ORDER = [("un", "O"), ("un", "C"), ("un", "I"), ("un", "D"), ("caps", "D")]
-S_ORDER = (gs("C", 0, 1024, 1600) + gs("D", 0, 512, 1024, 1280) + gs("I", 0, 1024, 2048) + [("pick", "I")]
-           + gs("O", 0, 1024, 2048))
-V_ORDER = ([("unA", "O"), ("unB", "O"), ("unA", "C"), ("unA", "I"), ("unB", "C"), ("unB", "I")] + gs("C", 1600, 2048)
-           + [("unA", "D"), ("flags", "D"), ("unB", "D")] + gs("D", 1280, 2048) + sc("D", 0, 512, 1024, 1536, 2048) + [("pick", "D")]
-           + sc("I", 0, 1024, 2048) + sc("C", 0, 1024, 2048) + [("pick", "C")] + sc("O", 0, 1024, 2048)
+S_ORDER = (gs("D", 512, 1024) + gs("D", 1536, 2048) + gs("C", 512, 1024) + gs("C", 1536, 2048)
+           + gs("I", 0, 640, 1344) + gs("O", 0, 704, 1344))
+V_ORDER = (gs("D", 0, 512) + gs("D", 1024, 1536) + gs("C", 0, 512) + gs("C", 1024, 1536) + gs("I", 1344, 2048)
+           + gs("O", 1344, 2048) + sc("I", 0, 640, 1344, 2048) + [("pick", "I")] + sc("O", 0, 704, 1344, 2048)
            + [("acc", "O"), ("fin", "O")])
-G_ORDER = ["ends", "C", "I", "relay", "PD", "PI", "PC"]
 
 SCRATCH = {
     "win": ("sbuf", [128, COLS + 2 * PAD], "bfloat16"),
@@ -39,48 +37,60 @@ SCRATCH = {
     "seli": ("sbuf", [128, 128], "int32"),
     "SEL": ("sbuf", [128, 128], "float32"),
     "cc": ("sbuf", [128, 8], "bfloat16"),
+    "XO": ("sbuf", [128, 18], "int32"),
+    "XH": ("sbuf", [128, 18], "int32"),
+    "EH": ("sbuf", [128, 2], "int32"),
     "E": ("sbuf", [128, 1], "int32"),
-    "hilo": ("sbuf", [128, 2], "int32"),
-    "hl": ("sbuf", [128, 2], "bfloat16"),
-    "ef": ("sbuf", [128, 8], "float32"),
+    "Z": ("sbuf", [128, 136], "float32"),
+    "ef": ("sbuf", [128, 2], "float32"),
+    "offH": ("sbuf", [128, 128], "uint16"),
+    "pkH": ("sbuf", [128, 8], "uint16"),
     "IH": ("sbuf", [128, 512], "bfloat16"),
     "IL": ("sbuf", [128, 512], "bfloat16"),
-    "LH": ("sbuf", [128, 512], "bfloat16"),
-    "RL": ("sbuf", [128, 512], "bfloat16"),
+    "FH": ("sbuf", [128, LEN], "bfloat16"),
+    "GH": ("sbuf", [128, LEN], "bfloat16"),
+    "SH": ("sbuf", [128, LEN + 8], "bfloat16"),
+    "PH": ("sbuf", [128, 128], "bfloat16"),
+    "QH": ("sbuf", [128, 128], "bfloat16"),
+    "PI": ("sbuf", [128, 128], "bfloat16"),
     "LD": ("sbuf", [128, 128], "bfloat16"),
     "LC": ("sbuf", [128, 128], "bfloat16"),
     "LI": ("sbuf", [128, 128], "bfloat16"),
     "acc": ("sbuf", [128, 128], "bfloat16"),
     "Y": ("sbuf", [128, 128], "bfloat16"),
     "psA": ("psum", [128, 2048], "float32"),
-    "psB": ("psum", [128, 2048], "float32"),
+    "psC": ("psum", [128, 1536], "float32"),
+    "psB": ("psum", [128, 512], "float32"),
 }
-SEMAPHORES = ["d_idx", "d_end", "d_y", "gate", "m_x", "m_win", "m_ih", "i_p", "i_mk", "i_sel", "i_il", "v_rep", "v_mka",
+SEMAPHORES = ["d_idx", "d_end", "d_y", "lx", "m_x", "m_win", "m_ih", "i_p", "i_mk", "i_sel", "i_il", "v_rep", "v_mka",
               "v_MK", "v_sela", "v_SEL", "v_pm", "v_c", "v_cn", "v_il1", "v_il2", "v_ih", "v_il", "loc", "r_LD", "r_LC", "r_LI",
-              "r_E", "v_acc", "v_Y", "hi", "hl", "lr"]
-SEMAPHORES += ["d_tab%d" % _k for _k in range(len(TABS))] + ["ps%d" % _k for _k in range(4)] + ["f%d" % _k for _k in range(4)]
+              "v_acc", "v_Y", "r_XH", "r_E", "efU", "ZU", "unU", "pkH", "offH", "m_sH", "v_PH", "v_QH", "v_PI"]
+SEMAPHORES += ["d_tab%d" % _k for _k in range(len(TABS))]
+SEMAPHORES += ["r_G%d" % _k for _k in range(len(PIECES))] + ["sH%d" % _k for _k in range(len(PIECES))]
+for _n in "OH":
+    SCRATCH["hilo" + _n] = ("sbuf", [128, 2], "int32")
+    SCRATCH["hl" + _n] = ("sbuf", [128, 2], "bfloat16")
+    SCRATCH["LH" + _n] = ("sbuf", [128, 512], "bfloat16")
+    SCRATCH["RL" + _n] = ("sbuf", [128, 512], "bfloat16")
+    SEMAPHORES += [_s + _n for _s in ("hi", "hl", "lr")]
+    SEMAPHORES += ["%s%s%d" % (_s, _n, _h) for _s in ("ps", "f") for _h in range(4)]
 for _q in "OCID":
-    SCRATCH["X" + _q] = ("sbuf", [128, 18], "int32")
-    SCRATCH["Z" + _q] = ("sbuf", [128, 136], "float32")
-    SCRATCH["off" + _q] = ("sbuf", [128, 128], "uint16")
-    SCRATCH["pk" + _q] = ("sbuf", [128, 8], "uint16")
+    SCRATCH["off" + _q] = ("sbuf", [128, 128 if _q in AWAY else 136], "uint16")
     SCRATCH["G" + _q] = ("sbuf", [128, LEN], "bfloat16")
-    SCRATCH["S" + _q] = ("sbuf", [128, LEN + 8], "bfloat16")
-    SEMAPHORES += ["m_s" + _q, "off" + _q, "pk" + _q, "ef" + _q, "Z" + _q, "un" + _q]
-    if _q in HLISTS:
+    SEMAPHORES += ["off" + _q, "r_off" + _q]
+    if _q not in AWAY:
+        SCRATCH["S" + _q] = ("sbuf", [128, LEN + 8], "bfloat16")
         SCRATCH["F" + _q] = ("sbuf", [128, LEN], "bfloat16")
-        SEMAPHORES += ["r_F%s0" % _q, "r_F%s1" % _q]
-    if _q != "O":
-        SCRATCH["P" + _q] = ("sbuf", [128, 128], "bfloat16")
-        SEMAPHORES += ["v_P" + _q, "r_" + _q]
+        SEMAPHORES += ["m_s" + _q, "r_F%s0" % _q, "r_F%s1" % _q]
 SEMAPHORES += ["g%s%d" % (_s[1], _s[2]) for _s in S_ORDER + V_ORDER if _s[0] == "g"]
 SEMAPHORES += ["s%s%d" % (_s[1], _s[2]) for _s in V_ORDER if _s[0] == "scan"]
 
 
 def helpers_of(core, T, topo):
     same = [k for k in range(core - 8, core + 9) if k >= 0 and topo.host(k) == topo.host(core) and topo.chip(k) == topo.chip(core)
-            and topo.die(k) == topo.die(core) and T.rank_of(k) is None]
-    return same[:len(HLISTS)]
+            and T.rank_of(k) is None]
+    same.sort(key=lambda k: topo.die(k) != topo.die(core))
+    return dict(zip(ROLES, same))
 
 
 def neighbours(core, T, topo):
@@ -97,56 +107,52 @@ def as_mask(which):
     return sum(1 << k for k in which)
 
 
-def ends_masks(rank, T, topo):
+def list_masks(rank, T, topo):
     i, c = neighbours(rank, T, topo)
-    out = engines(topo.mask(rank, helpers_of(c, T, topo)[HLISTS.index("C")]))
-    own = [k for k in engines(topo.mask(rank, helpers_of(rank, T, topo)[HLISTS.index("O")])) if k not in out]
+    out = engines(topo.mask(rank, helpers_of(c, T, topo)["C"]))
+    rest = [k for k in engines(topo.mask(rank, helpers_of(rank, T, topo)[HOME["O"]])) if k not in out]
     n = len(out) // 2
-    return {"C": as_mask(out[:n]), "I": as_mask(out[n:]), "O": as_mask(own[:n])}
+    return {"C": as_mask(out[:n]), "I": as_mask(out[n:]), "O": as_mask(rest)}
 
 
-def constants(g, T, topo, full):
+def unpack_constants(g, T, full):
     op, sem, v = AluOpType, T.sem, g.vector
-    cA, cB, cU, cW, cN, cV = [T.cc[:, k:k + 1] for k in range(6)]
-    g.iota(T.pcol[:], [[0, 8]], 0, 1).then_inc(sem.i_p, 1)
+    a = 0 if full else 128
     if full:
         g.iota(T.mki[:, 0:128], [[-1, 8], [0, 16]], 0, 1).then_inc(sem.i_mk, 1)
-        g.iota(T.mki[:, 128:136], [[-1, 8]], 0, 1).then_inc(sem.i_mk, 1)
-        g.iota(T.seli[:], [[0, 8], [-8, 16]], 0, 1).then_inc(sem.i_sel, 1)
-    g.iota(T.IL[:, 0:128], [[1, 128]], -256, 0, allow_small_or_imprecise_dtypes=True).then_inc(sem.i_il, 1)
+    g.iota(T.mki[:, 128:136], [[-1, 8]], 0, 1).then_inc(sem.i_mk, 1)
+    g.iota(T.seli[:], [[0, 8], [-8, 16]], 0, 1).then_inc(sem.i_sel, 1)
     if full:
-        v.memset(T.XO[0:1, 16:18], 0).then_inc(sem.m_x, 1)
-        v.memset(T.win[:, 0:PAD], -M).then_inc(sem.m_win, 1)
-        v.memset(T.win[:, PAD + COLS:PAD + COLS + PAD], -M).then_inc(sem.m_win, 1)
-    v.wait_ge(sem.i_p, 1)
-    if full:
+        v.wait_ge(sem.i_p, 1)
         v.tensor_scalar(T.pmod[:], T.pcol[:], 15, None, op.bitwise_and).then_inc(sem.v_pm, 1)
+    v.wait_ge(sem.i_mk, 2 if full else 1)
+    v.tensor_scalar(T.mki[:, a:136], T.mki[:, a:136], 7, None, op.bitwise_and).then_inc(sem.v_mka, 1)
+    v.wait_ge(sem.i_sel, 1)
+    v.tensor_scalar(T.seli[:], T.seli[:], 3, None, op.arith_shift_right).then_inc(sem.v_sela, 1)
+    if full:
+        v.wait_ge(sem.v_pm, 1)
+        v.tensor_copy(T.rep[:], T.pmod[:]).then_inc(sem.v_rep, 1)
+    v.wait_ge(sem.v_mka, 1)
+    v.tensor_scalar(T.MK[:, a:136], T.mki[:, a:136], 0.0, None, op.is_equal).then_inc(sem.v_MK, 1)
+    v.wait_ge(sem.v_sela, 1)
+    v.tensor_scalar(T.SEL[:], T.seli[:], 0.0, None, op.is_equal).then_inc(sem.v_SEL, 1)
+
+
+def cap_constants(g, T):
+    op, sem, v = AluOpType, T.sem, g.vector
+    cA, cB, cU, cW, cN, cV = [T.cc[:, k:k + 1] for k in range(6)]
+    v.wait_ge(sem.i_p, 1)
     v.tensor_scalar(cN, T.pcol[:, 0:1], 127.0, -5.0, op.is_equal, op.mult).then_inc(sem.v_cn, 1)
     v.tensor_scalar(cV, T.pcol[:, 0:1], 127.0, -556.0, op.is_lt, op.mult).then_inc(sem.v_cn, 1)
     v.tensor_scalar(cA, T.pcol[:, 0:1], 127.0, None, op.is_lt).then_inc(sem.v_c, 1)
     v.tensor_scalar(cB, T.pcol[:, 0:1], 127.0, 300.0, op.is_equal, op.mult).then_inc(sem.v_c, 1)
-    if full:
-        v.wait_ge(sem.v_pm, 1)
-        v.tensor_copy(T.rep[:], T.pmod[:]).then_inc(sem.v_rep, 1)
     v.wait_ge(sem.v_cn, 2)
     v.tensor_scalar(cU, cV, 300.0, None, op.add).then_inc(sem.v_c, 1)
     v.tensor_scalar(cW, cN, 4.0, None, op.add).then_inc(sem.v_c, 1)
-    if full:
-        v.wait_ge(sem.i_mk, 2)
-        v.tensor_scalar(T.mki[:], T.mki[:], 7, None, op.bitwise_and).then_inc(sem.v_mka, 1)
-        v.wait_ge(sem.i_sel, 1)
-        v.tensor_scalar(T.seli[:], T.seli[:], 3, None, op.arith_shift_right).then_inc(sem.v_sela, 1)
-        v.wait_ge(sem.v_mka, 1)
-        v.tensor_scalar(T.MK[:], T.mki[:], 0.0, None, op.is_equal).then_inc(sem.v_MK, 1)
-        v.wait_ge(sem.v_sela, 1)
-        v.tensor_scalar(T.SEL[:], T.seli[:], 0.0, None, op.is_equal).then_inc(sem.v_SEL, 1)
     for h in range(4):
         v.memset(T.IH[:, 128 * h:128 * h + 128], float(h - 256)).then_inc(sem.m_ih, 1)
     v.wait_ge(sem.i_il, 1)
     v.tensor_scalar(T.IL[:, 128:256], T.IL[:, 0:128], 128.0, None, op.add).then_inc(sem.v_il1, 1)
-    if full:
-        for q in "OCID":
-            v.memset(T["S" + q][:, 0:1], 0.0).then_inc(sem["m_s" + q], 1)
     v.wait_ge(sem.v_il1, 1)
     v.tensor_scalar(T.IL[:, 256:512], T.IL[:, 0:256], 256.0, None, op.add).then_inc(sem.v_il2, 1)
     v.wait_ge(sem.m_ih, 4)
@@ -154,70 +160,174 @@ def constants(g, T, topo, full):
     v.tensor_scalar(T.IH[:], T.IH[:], cA, cB, op.mult, op.add).then_inc(sem.v_ih, 1)
     v.wait_ge(sem.v_il2, 1)
     v.tensor_scalar(T.IL[:], T.IL[:], cA, cB, op.mult, op.add).then_inc(sem.v_il, 1)
-
-
-def factors(v, T, end):
-    op, sem = AluOpType, T.sem
-    v.tensor_scalar(T.hilo[:, 0:1], end, 9, None, op.arith_shift_right).then_inc(sem.hi, 1)
-    v.tensor_scalar(T.hilo[:, 1:2], end, 511, None, op.bitwise_and).then_inc(sem.hi, 1)
-    v.wait_ge(sem.hi, 2)
-    v.wait_ge(sem.v_c, 4)
-    v.tensor_scalar(T.hl[:], T.hilo[:], T.cc[:, 0:1], T.cc[:, 2:3], op.mult, op.add).then_inc(sem.hl, 1)
     v.wait_ge(sem.v_ih, 1)
     v.wait_ge(sem.v_il, 1)
-    v.wait_ge(sem.hl, 1)
-    v.tensor_scalar(T.LH[:], T.IH[:], T.hl[:, 0:1], -M, op.is_equal, op.mult).then_inc(sem.lr, 1)
-    v.tensor_scalar(T.RL[:], T.IL[:], T.hl[:, 1:2], T.cc[:, 3:4], op.is_equal, op.mult).then_inc(sem.lr, 1)
 
 
-def caps(t, T):
-    t.wait_ge(T.sem.lr, 2)
+def bank(T, n, h):
+    return T.psA[:, 512 * h:512 * h + 512] if n == "H" else T.psC[:, 512 * (h % 3):512 * (h % 3) + 512]
+
+
+def factors(g, T, end, n):
+    op, sem, v, t = AluOpType, T.sem, g.vector, g.tensor
+    hilo, hl, LH, RL = T["hilo" + n], T["hl" + n], T["LH" + n], T["RL" + n]
+    v.tensor_scalar(hilo[:, 0:1], end, 9, None, op.arith_shift_right).then_inc(sem["hi" + n], 1)
+    v.tensor_scalar(hilo[:, 1:2], end, 511, None, op.bitwise_and).then_inc(sem["hi" + n], 1)
+    v.wait_ge(sem["hi" + n], 2)
+    v.tensor_scalar(hl[:], hilo[:], T.cc[:, 0:1], T.cc[:, 2:3], op.mult, op.add).then_inc(sem["hl" + n], 1)
+    v.wait_ge(sem["hl" + n], 1)
+    v.tensor_scalar(LH[:], T.IH[:], hl[:, 0:1], -M, op.is_equal, op.mult).then_inc(sem["lr" + n], 1)
+    v.tensor_scalar(RL[:], T.IL[:], hl[:, 1:2], T.cc[:, 3:4], op.is_equal, op.mult).then_inc(sem["lr" + n], 1)
+    t.wait_ge(sem["lr" + n], 2)
     for h in range(4):
-        t.matmul(T.psA[:, 512 * h:512 * h + 512], T.LH[:, 128 * h:128 * h + 128], T.RL[:], True, True
-                 ).then_inc(T.sem["ps%d" % h], 1)
+        if n == "O" and h == 3:
+            t.wait_ge(sem.fO0, 1)
+        t.matmul(bank(T, n, h), LH[:, 128 * h:128 * h + 128], RL[:], True, True).then_inc(sem["ps%s%d" % (n, h)], 1)
+
+
+def copy_caps(g, T, F, n):
+    sem, v, s = T.sem, g.vector, g.scalar
+    for h in range(4):
+        e = v if n == "H" and h % 2 else s
+        e.wait_ge(sem["ps%s%d" % (n, h)], 1)
+        out, src = F[:, 512 * h:512 * h + 512], bank(T, n, h)
+        (s.activation(out, src, ActivationFunctionType.Copy) if e is s else v.tensor_copy(out, src)
+         ).then_inc(sem["f%s%d" % (n, h)], 1)
+
+
+def unpack(g, T, ent, end, before, waits):
+    op, sem, v, t = AluOpType, T.sem, g.vector, g.tensor
+    for name, n in waits:
+        v.wait_ge(sem[name], n)
+    v.tensor_copy(T.ef[:, 0:1], end).then_inc(sem.efU, 1)
+    v.tensor_tensor(T.ef[:, 1:2], end, before, op.not_equal).then_inc(sem.efU, 1)
+    v.wait_ge(sem.v_MK, 1)
+    a, n = 128, 1
+    if ent is not None:
+        a, n = 0, 2
+        v.wait_ge(sem.v_rep, 1)
+        v.tensor_tensor(T.Z[:, 0:128], ent.indirect(T.rep[:]), T.MK[:, 0:128], op.mult).then_inc(sem.ZU, 1)
+    v.wait_ge(sem.efU, 2)
+    v.tensor_scalar(T.Z[:, 128:136], T.MK[:, 128:136], T.ef[:, 0:1], T.ef[:, 1:2], op.mult, op.mult).then_inc(sem.ZU, 1)
+    t.wait_ge(sem.v_SEL, 1)
+    t.wait_ge(sem.ZU, n)
+    t.matmul(T.psB[:, a:136], T.SEL[:], T.Z[:, a:136], True, True).then_inc(sem.unU, 1)
+
+
+def offsets(g, T, rank, out, done):
+    op = AluOpType
+    g.vector.tensor_scalar(out, T.psB[:, 0:128], float(PAD - rank * COLS), float(PAD + COLS), op.add, op.min).then_inc(done, 1)
 
 
 def helper_program(g, core, main, q, T, topo):
-    sem, v, s = T.sem, g.vector, g.scalar
+    op, sem, v = AluOpType, T.sem, g.vector
     i, c = neighbours(main, T, topo)
-    owner = {"O": main, "C": c, "I": i}[q]
-    constants(g, T, topo, False)
-    v.wait_ge(sem.r_E, len(engines(ends_masks(owner, T, topo)[q])))
-    factors(v, T, T.E[:])
-    caps(g.tensor, T)
-    F = T["F" + q]
-    for h in range(4):
-        e = v if h % 2 else s
-        e.wait_ge(sem["ps%d" % h], 1)
-        out, src = F[:, 512 * h:512 * h + 512], T.psA[:, 512 * h:512 * h + 512]
-        (s.activation(out, src, ActivationFunctionType.Copy) if e is s else v.tensor_copy(out, src)).then_inc(sem["f%d" % h], 1)
-    mask = topo.mask(core, main)
-    rid, pid = topo.addr(main, core)
-    for k in range(2):
-        g.wait_ge(sem["f%d" % (2 * k)], 1)
-        g.wait_ge(sem["f%d" % (2 * k + 1)], 1)
-        part = F[:, 1024 * k:1024 * k + 1024]
-        g.remote_dma(out_ap=part, in_ap=part, remote_sem=sem["r_F%s%d" % (q, k)], local_sem=sem.loc, pid=pid, routing_id=rid,
-                     dma_engine_mask=mask)
-    g.wait_ge(sem.loc, 2 * len(engines(mask)))
+    sent = []
+
+    def send(dst, out, src, rsem):
+        rid, pid = topo.addr(dst, core)
+        mask = topo.mask(core, dst)
+        g.remote_dma(out_ap=out, in_ap=src, remote_sem=rsem, local_sem=sem.loc, pid=pid, routing_id=rid, dma_engine_mask=mask)
+        sent.append(len(engines(mask)))
+
+    def send_caps(p, F, n):
+        for k in range(2):
+            g.wait_ge(sem["f%s%d" % (n, 2 * k)], 1)
+            g.wait_ge(sem["f%s%d" % (n, 2 * k + 1)], 1)
+            a = 1024 * k
+            send(main, T["F" + p][:, a:a + 1024], F[:, a:a + 1024], sem["r_F%s%d" % (p, k)])
+
+    g.iota(T.pcol[:], [[0, 8]], 0, 1).then_inc(sem.i_p, 1)
+    g.iota(T.IL[:, 0:128], [[1, 128]], -256, 0, allow_small_or_imprecise_dtypes=True).then_inc(sem.i_il, 1)
+    if q == "D":
+        cap_constants(g, T)
+        unpack_constants(g, T, False)
+    else:
+        unpack_constants(g, T, True)
+        cap_constants(g, T)
+    if q in AWAY:
+        v.memset(T.SH[:, 0:1], 0.0).then_inc(sem.m_sH, 1)
+    if q == HOME["O"]:
+        v.wait_ge(sem.r_E, len(engines(list_masks(main, T, topo)["O"])))
+        factors(g, T, T.E[:], "O")
+        copy_caps(g, T, T.FO, "O")
+        send_caps("O", T.FO, "O")
+
+    if q == "D":
+        end, before = T.EH[:, 0:1], T.EH[:, 1:2]
+        unpack(g, T, None, end, before, [("r_XH", len(engines(topo.mask(helpers_of(i, T, topo)["C"], core))))])
+    else:
+        end, before = T.XH[:, 16:17], T.XH[:, 17:18]
+        nx = len(engines(list_masks(c if q == "C" else i, T, topo)[q]))
+        if q == "C":
+            g.wait_ge(sem.r_XH, nx)
+            send(helpers_of(i, T, topo)["D"], T.EH[:], T.XH[:, 16:18], sem.r_XH)
+        unpack(g, T, T.XH[:, 0:16], end, before, [("r_XH", nx)])
+        v.wait_ge(sem.unU, 1)
+        if q == "C":
+            offsets(g, T, T.rank_of(i), T.offH[:], sem.offH)
+            offsets(g, T, T.rank_of(main), T.offC[:], sem.offC)
+            g.wait_ge(sem.offH, 1)
+            send(i, T.offD[:], T.offH[:], sem.r_offD)
+            g.wait_ge(sem.offC, 1)
+            send(main, T.offC[:], T.offC[:], sem.r_offC)
+        else:
+            offsets(g, T, T.rank_of(main), T.offI[:, 0:128], sem.offI)
+            v.tensor_copy(T.offI[:, 128:136], T.psB[:, 128:136]).then_inc(sem.offI, 1)
+            g.wait_ge(sem.offI, 2)
+            send(main, T.offI[:], T.offI[:], sem.r_offI)
+    factors(g, T, end, "H")
+    if q in AWAY:
+        if q == "D":
+            v.wait_ge(sem.unU, 1)
+        v.tensor_copy(T.pkH[:], T.psB[:, 128:136]).then_inc(sem.pkH, 1)
+    copy_caps(g, T, T.FH, "H")
+    if q not in AWAY:
+        send_caps(q, T.FH, "H")
+        g.wait_ge(sem.loc, sum(sent))
+        return
+
+    ng = len(engines(topo.mask(main, core)))
+    for k, (a, b) in enumerate(PIECES):
+        for h in range(a // 512, b // 512):
+            v.wait_ge(sem["fH%d" % h], 1)
+        v.wait_ge(sem["r_G%d" % k], ng)
+        if k:
+            v.wait_ge(sem["sH%d" % (k - 1)], 1)
+        v.tensor_tensor_scan(T.SH[:, a + 1:b + 1], T.FH[:, a:b], T.GH[:, a:b], -M if a == 0 else T.SH[:, a:a + 1], op.min, op.max
+                             ).then_inc(sem["sH%d" % k], 1)
+    v.wait_ge(sem.m_sH, 1)
+    v.wait_ge(sem.pkH, 1)
+    v.wait_ge(sem["sH%d" % (len(PIECES) - 1)], 1)
+    v.tensor_copy(T.PH[:], T.SH[:, 0:LEN + 1].indirect(T.pkH[:])).then_inc(sem.v_PH, 1)
+    if q == "D":
+        g.wait_ge(sem.v_PH, 1)
+        send(helpers_of(i, T, topo)["C"], T.LD[:], T.PH[:], sem.r_LD)
+    else:
+        v.wait_ge(sem.v_PH, 1)
+        v.wait_ge(sem.r_LD, len(engines(topo.mask(helpers_of(i, T, topo)["D"], core))))
+        v.tensor_tensor(T.QH[:], T.PH[:], T.LD[:], op.max).then_inc(sem.v_QH, 1)
+        g.wait_ge(sem.v_QH, 1)
+        send(c, T.LC[:], T.QH[:], sem.r_LC)
+    g.wait_ge(sem.loc, sum(sent))
 
 
 def rank_program(g, core, T, topo):
     for r in T.cores:
-        hs = helpers_of(r, T, topo)
-        if core in hs:
-            helper_program(g, core, r, HLISTS[hs.index(core)], T, topo)
+        for q, h in helpers_of(r, T, topo).items():
+            if core == h:
+                helper_program(g, core, r, q, T, topo)
     if T.rank_of(core) is None:
         return
     op, fn, sem = AluOpType, ActivationFunctionType, T.sem
-    v, s, t, y = g.vector, g.scalar, g.tensor, g.sync
-    base = T.rank_of(core) * COLS
+    v, s, y = g.vector, g.scalar, g.sync
     i, c = neighbours(core, T, topo)
-    mi, mc = topo.mask(core, i), topo.mask(core, c)
-    ni, nc = len(engines(mi)), len(engines(mc))
-    helpers = helpers_of(core, T, topo)
-    nf = {q: len(engines(topo.mask(h, core))) for q, h in zip(HLISTS, helpers)}
-    arrive = {"C": nc, "I": ni, "D": ni}
+    H, Hi, Hc = helpers_of(core, T, topo), helpers_of(i, T, topo), helpers_of(c, T, topo)
+    masks = list_masks(core, T, topo)
+    nf = {q: len(engines(topo.mask(H[HOME[q]], core))) for q in HOME}
+    ready = {"O": ("offO", 2)}
+    for q, h in (("C", H["C"]), ("I", H["I"]), ("D", Hi["C"])):
+        ready[q] = ("r_off" + q, len(engines(topo.mask(h, core))))
     sent = []
 
     def send(dst, mask, out, src, rsem):
@@ -226,6 +336,7 @@ def rank_program(g, core, T, topo):
         sent.append(len(engines(mask)))
 
     y.dma_start(T.XO[:, 0:16], T.idx[:]).then_inc(sem.d_idx, 16)
+    v.memset(T.XO[0:1, 16:18], 0).then_inc(sem.m_x, 1)
     y.wait_ge(sem.m_x, 1)
     y.dma_start(T.XO[1:8, 17:18], T.end[15:16, 0:7]).then_inc(sem.d_end, 16)
     s.wait_ge(sem.m_x, 1)
@@ -233,24 +344,21 @@ def rank_program(g, core, T, topo):
     s.dma_start(T.XO[8:128, 17:18], T.end[0:15, :]).then_inc(sem.d_end, 16)
     a = 0
     for n, w in enumerate(TABS):
-        e = s
-        if GATE and n >= GATE:
-            e = y
-            if n == GATE:
-                y.wait_ge(sem.gate, 1)
-        e.dma_start(T.win[:, PAD + a:PAD + a + w], T.tab[:, a:a + w]).then_inc(sem["d_tab%d" % n], 16)
+        if n == 1:
+            y.wait_ge(sem.lx, len(engines(masks["C"] | masks["I"])))
+        (y if n else s).dma_start(T.win[:, PAD + a:PAD + a + w], T.tab[:, a:a + w]).then_inc(sem["d_tab%d" % n], 16)
         a += w
 
-    constants(g, T, topo, True)
-
-    t.wait_ge(sem.v_SEL, 1)
-    for what, q in T_ORDER:
-        if what == "caps":
-            caps(t, T)
-        else:
-            t.wait_ge(sem["Z" + q], 2)
-            k = 512 * BANK[q]
-            t.matmul(T.psB[:, k:k + 136], T.SEL[:], T["Z" + q][:], True, True).then_inc(sem["un" + q], 1)
+    v.memset(T.win[:, 0:PAD], -M).then_inc(sem.m_win, 1)
+    v.memset(T.win[:, PAD + COLS:PAD + COLS + PAD], -M).then_inc(sem.m_win, 1)
+    g.iota(T.pcol[:], [[0, 8]], 0, 1).then_inc(sem.i_p, 1)
+    for q in "OI":
+        v.memset(T["S" + q][:, 0:1], 0.0).then_inc(sem["m_s" + q], 1)
+    unpack_constants(g, T, True)
+    unpack(g, T, T.XO[:, 0:16], T.XO[:, 16:17], T.XO[:, 17:18], [("m_x", 1), ("d_idx", 16), ("d_end", 48)])
+    v.wait_ge(sem.unU, 1)
+    offsets(g, T, T.rank_of(core), T.offO[:, 0:128], sem.offO)
+    v.tensor_copy(T.offO[:, 128:136], T.psB[:, 128:136]).then_inc(sem.offO, 1)
 
     scans, gathers = {}, {}
     for st in S_ORDER + V_ORDER:
@@ -265,38 +373,11 @@ def rank_program(g, core, T, topo):
             waited[eng, name] = 1
             e.wait_ge(sem[name], n)
 
-    def arrived(q):
-        if q == "O":
-            wait(v, "v", "d_idx", 16)
-            wait(v, "v", "d_end", 48)
-            wait(v, "v", "m_x", 1)
-        else:
-            wait(v, "v", "r_" + q, arrive[q])
-
-    def unA(q):
-        X, k = T["X" + q], 2 * "OCID".index(q)
-        end, ne = T.ef[:, k:k + 1], T.ef[:, k + 1:k + 2]
-        arrived(q)
-        wait(v, "v", "v_rep", 1)
-        wait(v, "v", "v_MK", 1)
-        v.tensor_copy(end, X[:, 16:17]).then_inc(sem["ef" + q], 1)
-        v.tensor_tensor(ne, X[:, 16:17], X[:, 17:18], op.not_equal).then_inc(sem["ef" + q], 1)
-        v.tensor_tensor(T["Z" + q][:, 0:128], X[:, 0:16].indirect(T.rep[:]), T.MK[:, 0:128], op.mult).then_inc(sem["Z" + q], 1)
-        wait(v, "v", "ef" + q, 2)
-        v.tensor_scalar(T["Z" + q][:, 128:136], T.MK[:, 128:136], end, ne, op.mult, op.mult).then_inc(sem["Z" + q], 1)
-
-    def unB(q):
-        k = 512 * BANK[q]
-        wait(v, "v", "un" + q, 1)
-        v.tensor_scalar(T["off" + q][:], T.psB[:, k:k + 128], float(PAD - base), float(PAD + COLS), op.add, op.min
-                        ).then_inc(sem["off" + q], 1)
-        v.tensor_copy(T["pk" + q][:], T.psB[:, k + 128:k + 136]).then_inc(sem["pk" + q], 1)
-
     def gath(e, eng, q, a, b):
         for k in range(len(TABS)):
             wait(e, eng, "d_tab%d" % k, 16)
         wait(e, eng, "m_win", 2)
-        wait(e, eng, "off" + q, 1)
+        wait(e, eng, *ready[q])
         src, out = T.win[:].indirect(T["off" + q][:, a // 16:b // 16]), T["G" + q][:, a:b]
         ins = s.activation(out, src, fn.Copy) if eng == "s" else v.tensor_copy(out, src)
         ins.then_inc(sem["g%s%d" % (q, a)], 1)
@@ -306,88 +387,59 @@ def rank_program(g, core, T, topo):
         for a2, b2 in gathers[q]:
             if a2 < b and b2 > a:
                 wait(v, "v", "g%s%d" % (q, a2), 1)
-        if q in HLISTS:
-            for k in range(a // 1024, (b + 1023) // 1024):
-                wait(v, "v", "r_F%s%d" % (q, k), nf[q])
-        else:
-            for h in range(a // 512, (b + 511) // 512):
-                wait(v, "v", "ps%d" % h, 1)
+        for k in range(a // 1024, (b + 1023) // 1024):
+            wait(v, "v", "r_F%s%d" % (q, k), nf[q])
         for a2, b2 in scans[q]:
             if b2 == a:
                 wait(v, "v", "s%s%d" % (q, a2), 1)
-        cap = T["F" + q] if q in HLISTS else T.psA
-        v.tensor_tensor_scan(S[:, a + 1:b + 1], cap[:, a:b], T["G" + q][:, a:b], -M if a == 0 else S[:, a:a + 1], op.min, op.max
-                             ).then_inc(sem["s%s%d" % (q, a)], 1)
+        v.tensor_tensor_scan(S[:, a + 1:b + 1], T["F" + q][:, a:b], T["G" + q][:, a:b], -M if a == 0 else S[:, a:a + 1],
+                             op.min, op.max).then_inc(sem["s%s%d" % (q, a)], 1)
 
-    def picked(e, eng, q):
-        wait(e, eng, "s%s%d" % (q, scans[q][-1][0]), 1)
-        wait(e, eng, "m_s" + q, 1)
-        wait(e, eng, "pk" + q, 1)
-        return T["S" + q][:, 0:LEN + 1].indirect(T["pk" + q][:])
+    def picked(q):
+        wait(v, "v", "s%s%d" % (q, scans[q][-1][0]), 1)
+        wait(v, "v", "m_s" + q, 1)
+        wait(v, "v", *ready[q])
+        return T["S" + q][:, 0:LEN + 1].indirect(T["off" + q][:, 128:136])
 
     for st in V_ORDER:
         what, q = st[0], st[1]
-        if what == "unA":
-            unA(q)
-        elif what == "unB":
-            unB(q)
-        elif what == "flags":
-            arrived(q)
-            factors(v, T, T.XD[:, 16:17])
-        elif what == "g":
+        if what == "g":
             gath(v, "v", q, st[2], st[3])
         elif what == "scan":
             scan(q, st[2], st[3])
         elif what == "pick":
-            v.tensor_copy(T["P" + q][:], picked(v, "v", q)).then_inc(sem["v_P" + q], 1)
+            v.tensor_copy(T.PI[:], picked(q)).then_inc(sem.v_PI, 1)
         elif what == "acc":
-            src = picked(v, "v", q)
-            v.wait_ge(sem.r_LI, ni)
+            src = picked(q)
+            v.wait_ge(sem.r_LI, len(engines(topo.mask(i, core))))
             v.tensor_tensor(T.acc[:], src, T.LI[:], op.max).then_inc(sem.v_acc, 1)
         else:
             v.wait_ge(sem.v_acc, 1)
-            v.wait_ge(sem.r_LC, nc)
+            v.wait_ge(sem.r_LC, len(engines(topo.mask(Hc["C"], core))))
             v.tensor_tensor(T.Y[:], T.acc[:], T.LC[:], op.max).then_inc(sem.v_Y, 1)
 
     for st in S_ORDER:
-        if st[0] == "pick":
-            s.activation(T["P" + st[1]][:], picked(s, "s", st[1]), fn.Copy).then_inc(sem["v_P" + st[1]], 1)
-        else:
-            gath(s, "s", st[1], st[2], st[3])
+        gath(s, "s", st[1], st[2], st[3])
 
     for name, n in (("d_idx", 16), ("d_end", 48), ("m_x", 1)):
         g.wait_ge(sem[name], n)
-    for what in G_ORDER:
-        if what == "C":
-            send(c, mc, T.XC[:], T.XO[:], sem.r_C)
-            if GATE:
-                g.sem_inc(sem.gate, 1)
-        elif what == "I":
-            send(i, mi, T.XI[:], T.XO[:], sem.r_I)
-        elif what == "ends":
-            masks, calls = ends_masks(core, T, topo), []
-            for q, r in (("C", c), ("I", i), ("O", core)):
-                rid, pid = topo.addr(helpers_of(r, T, topo)[HLISTS.index(q)], core)
-                calls.append(RemoteDMATransfer(dst_ids=[DstId(rid=rid, pnc=pid)], dma_engine_mask=masks[q], remote_sem=sem.r_E,
-                                               srcs=[T.XO[:, 16:17]], dsts=[T.E[:]]))
-                sent.append(len(engines(masks[q])))
-            g.remote_dma_fused(calls, local_sem=sem.loc)
-        elif what == "relay":
-            g.wait_ge(sem.r_C, nc)
-            send(i, mi, T.XD[:], T.XC[:], sem.r_D)
-        elif what == "PD":
-            g.wait_ge(sem.v_PD, 1)
-            send(i, mi, T.LD[:], T.PD[:], sem.r_LD)
-        elif what == "PI":
-            g.wait_ge(sem.v_PI, 1)
-            send(i, mi, T.LI[:], T.PI[:], sem.r_LI)
-        else:
-            g.wait_ge(sem.v_PC, 1)
-            g.wait_ge(sem.r_LD, ni)
-            rid, pid = topo.addr(c, core)
-            g.remote_dma_fused([RemoteDMATransfer(dst_ids=[DstId(rid=rid, pnc=pid)], dma_engine_mask=mc, remote_sem=sem.r_LC,
-                                                  srcs=[T.PC[:], T.LD[:]], dsts=[T.LC[:]], alu_op=2)], local_sem=sem.loc)
-            sent.append(nc)
+    calls = []
+    for dst, mask in ((Hc["C"], masks["C"]), (Hi["I"], masks["I"])):
+        rid, pid = topo.addr(dst, core)
+        calls.append(RemoteDMATransfer(dst_ids=[DstId(rid=rid, pnc=pid)], dma_engine_mask=mask, remote_sem=sem.r_XH,
+                                       srcs=[T.XO[:]], dsts=[T.XH[:]]))
+    g.remote_dma_fused(calls, local_sem=sem.lx)
+    send(H[HOME["O"]], masks["O"], T.E[:], T.XO[:, 16:17], sem.r_E)
+    for q in "DC":
+        done = set()
+        for k, (a, b) in enumerate(PIECES):
+            for a2, b2 in gathers[q]:
+                if a2 < b and b2 > a and a2 not in done:
+                    done.add(a2)
+                    g.wait_ge(sem["g%s%d" % (q, a2)], 1)
+            send(H[q], topo.mask(core, H[q]), T.GH[:, a:b], T["G" + q][:, a:b], sem["r_G%d" % k])
+    g.wait_ge(sem.v_PI, 1)
+    send(i, topo.mask(core, i), T.LI[:], T.PI[:], sem.r_LI)
     g.wait_ge(sem.loc, sum(sent))
 
     y.wait_ge(sem.v_Y, 1)

import numpy as np
from concourse.bass import DstId, RemoteDMATransfer
from concourse.mybir import dt, AluOpType, AxisListType, ActivationFunctionType

M = 9.953037915854457e+29
COLS = 8192
PAD = 8
LEN = 2048
TABS = [2048, 6144]
ROLES = "CDI"
HOME = {"O": "D", "I": "I"}
AWAY = "CD"
PIECES = [(0, 1024), (1024, 2048)]


def gs(q, *cuts):
    return [("g", q, a, b) for a, b in zip(cuts, cuts[1:])]


def sc(q, *cuts):
    return [("scan", q, a, b) for a, b in zip(cuts, cuts[1:])]


S_ORDER = (gs("D", 512, 1024) + gs("D", 1536, 2048) + gs("C", 512, 1024) + gs("C", 1536, 2048)
           + gs("I", 0, 640, 1344) + gs("O", 0, 704, 1344))
V_ORDER = (gs("D", 0, 512) + gs("D", 1024, 1536) + gs("C", 0, 512) + gs("C", 1024, 1536) + gs("I", 1344, 2048)
           + gs("O", 1344, 2048) + sc("I", 0, 640, 1344, 2048) + [("pick", "I")] + sc("O", 0, 704, 1344, 2048)
           + [("acc", "O"), ("fin", "O")])

SCRATCH = {
    "win": ("sbuf", [128, COLS + 2 * PAD], "bfloat16"),
    "pcol": ("sbuf", [128, 8], "int32"),
    "pmod": ("sbuf", [128, 8], "int32"),
    "rep": ("sbuf", [128, 8], "uint16"),
    "mki": ("sbuf", [128, 136], "int32"),
    "MK": ("sbuf", [128, 136], "float32"),
    "seli": ("sbuf", [128, 128], "int32"),
    "SEL": ("sbuf", [128, 128], "float32"),
    "cc": ("sbuf", [128, 8], "bfloat16"),
    "XO": ("sbuf", [128, 18], "int32"),
    "XH": ("sbuf", [128, 18], "int32"),
    "EH": ("sbuf", [128, 2], "int32"),
    "E": ("sbuf", [128, 1], "int32"),
    "Z": ("sbuf", [128, 136], "float32"),
    "ef": ("sbuf", [128, 2], "float32"),
    "offH": ("sbuf", [128, 128], "uint16"),
    "pkH": ("sbuf", [128, 8], "uint16"),
    "IH": ("sbuf", [128, 512], "bfloat16"),
    "IL": ("sbuf", [128, 512], "bfloat16"),
    "FH": ("sbuf", [128, LEN], "bfloat16"),
    "GH": ("sbuf", [128, LEN], "bfloat16"),
    "SH": ("sbuf", [128, LEN + 8], "bfloat16"),
    "PH": ("sbuf", [128, 128], "bfloat16"),
    "QH": ("sbuf", [128, 128], "bfloat16"),
    "PI": ("sbuf", [128, 128], "bfloat16"),
    "LD": ("sbuf", [128, 128], "bfloat16"),
    "LC": ("sbuf", [128, 128], "bfloat16"),
    "LI": ("sbuf", [128, 128], "bfloat16"),
    "acc": ("sbuf", [128, 128], "bfloat16"),
    "Y": ("sbuf", [128, 128], "bfloat16"),
    "psA": ("psum", [128, 2048], "float32"),
    "psC": ("psum", [128, 1536], "float32"),
    "psB": ("psum", [128, 512], "float32"),
}
SEMAPHORES = ["d_idx", "d_end", "d_y", "lx", "m_x", "m_win", "m_ih", "i_p", "i_mk", "i_sel", "i_il", "v_rep", "v_mka",
              "v_MK", "v_sela", "v_SEL", "v_pm", "v_c", "v_cn", "v_il1", "v_il2", "v_ih", "v_il", "loc", "r_LD", "r_LC", "r_LI",
              "v_acc", "v_Y", "r_XH", "r_E", "efU", "ZU", "unU", "pkH", "offH", "m_sH", "v_PH", "v_QH", "v_PI"]
SEMAPHORES += ["d_tab%d" % _k for _k in range(len(TABS))]
SEMAPHORES += ["r_G%d" % _k for _k in range(len(PIECES))] + ["sH%d" % _k for _k in range(len(PIECES))]
for _n in "OH":
    SCRATCH["hilo" + _n] = ("sbuf", [128, 2], "int32")
    SCRATCH["hl" + _n] = ("sbuf", [128, 2], "bfloat16")
    SCRATCH["LH" + _n] = ("sbuf", [128, 512], "bfloat16")
    SCRATCH["RL" + _n] = ("sbuf", [128, 512], "bfloat16")
    SEMAPHORES += [_s + _n for _s in ("hi", "hl", "lr")]
    SEMAPHORES += ["%s%s%d" % (_s, _n, _h) for _s in ("ps", "f") for _h in range(4)]
for _q in "OCID":
    SCRATCH["off" + _q] = ("sbuf", [128, 128 if _q in AWAY else 136], "uint16")
    SCRATCH["G" + _q] = ("sbuf", [128, LEN], "bfloat16")
    SEMAPHORES += ["off" + _q, "r_off" + _q]
    if _q not in AWAY:
        SCRATCH["S" + _q] = ("sbuf", [128, LEN + 8], "bfloat16")
        SCRATCH["F" + _q] = ("sbuf", [128, LEN], "bfloat16")
        SEMAPHORES += ["m_s" + _q, "r_F%s0" % _q, "r_F%s1" % _q]
SEMAPHORES += ["g%s%d" % (_s[1], _s[2]) for _s in S_ORDER + V_ORDER if _s[0] == "g"]
SEMAPHORES += ["s%s%d" % (_s[1], _s[2]) for _s in V_ORDER if _s[0] == "scan"]


def helpers_of(core, T, topo):
    same = [k for k in range(core - 8, core + 9) if k >= 0 and topo.host(k) == topo.host(core) and topo.chip(k) == topo.chip(core)
            and T.rank_of(k) is None]
    same.sort(key=lambda k: topo.die(k) != topo.die(core))
    return dict(zip(ROLES, same))


def neighbours(core, T, topo):
    near = [k for k in T.cores if k != core and topo.may_write(core, k)]
    i = [k for k in near if topo.rack(topo.host(k)) == topo.rack(topo.host(core))][0]
    return i, [k for k in near if k != i][0]


def engines(mask):
    return [k for k in range(16) if mask >> k & 1]


def as_mask(which):
    return sum(1 << k for k in which)


def list_masks(rank, T, topo):
    i, c = neighbours(rank, T, topo)
    out = engines(topo.mask(rank, helpers_of(c, T, topo)["C"]))
    rest = [k for k in engines(topo.mask(rank, helpers_of(rank, T, topo)[HOME["O"]])) if k not in out]
    n = len(out) // 2
    return {"C": as_mask(out[:n]), "I": as_mask(out[n:]), "O": as_mask(rest)}


def unpack_constants(g, T, full):
    op, sem, v = AluOpType, T.sem, g.vector
    a = 0 if full else 128
    if full:
        g.iota(T.mki[:, 0:128], [[-1, 8], [0, 16]], 0, 1).then_inc(sem.i_mk, 1)
    g.iota(T.mki[:, 128:136], [[-1, 8]], 0, 1).then_inc(sem.i_mk, 1)
    g.iota(T.seli[:], [[0, 8], [-8, 16]], 0, 1).then_inc(sem.i_sel, 1)
    if full:
        v.wait_ge(sem.i_p, 1)
        v.tensor_scalar(T.pmod[:], T.pcol[:], 15, None, op.bitwise_and).then_inc(sem.v_pm, 1)
    v.wait_ge(sem.i_mk, 2 if full else 1)
    v.tensor_scalar(T.mki[:, a:136], T.mki[:, a:136], 7, None, op.bitwise_and).then_inc(sem.v_mka, 1)
    v.wait_ge(sem.i_sel, 1)
    v.tensor_scalar(T.seli[:], T.seli[:], 3, None, op.arith_shift_right).then_inc(sem.v_sela, 1)
    if full:
        v.wait_ge(sem.v_pm, 1)
        v.tensor_copy(T.rep[:], T.pmod[:]).then_inc(sem.v_rep, 1)
    v.wait_ge(sem.v_mka, 1)
    v.tensor_scalar(T.MK[:, a:136], T.mki[:, a:136], 0.0, None, op.is_equal).then_inc(sem.v_MK, 1)
    v.wait_ge(sem.v_sela, 1)
    v.tensor_scalar(T.SEL[:], T.seli[:], 0.0, None, op.is_equal).then_inc(sem.v_SEL, 1)


def cap_constants(g, T):
    op, sem, v = AluOpType, T.sem, g.vector
    cA, cB, cU, cW, cN, cV = [T.cc[:, k:k + 1] for k in range(6)]
    v.wait_ge(sem.i_p, 1)
    v.tensor_scalar(cN, T.pcol[:, 0:1], 127.0, -5.0, op.is_equal, op.mult).then_inc(sem.v_cn, 1)
    v.tensor_scalar(cV, T.pcol[:, 0:1], 127.0, -556.0, op.is_lt, op.mult).then_inc(sem.v_cn, 1)
    v.tensor_scalar(cA, T.pcol[:, 0:1], 127.0, None, op.is_lt).then_inc(sem.v_c, 1)
    v.tensor_scalar(cB, T.pcol[:, 0:1], 127.0, 300.0, op.is_equal, op.mult).then_inc(sem.v_c, 1)
    v.wait_ge(sem.v_cn, 2)
    v.tensor_scalar(cU, cV, 300.0, None, op.add).then_inc(sem.v_c, 1)
    v.tensor_scalar(cW, cN, 4.0, None, op.add).then_inc(sem.v_c, 1)
    for h in range(4):
        v.memset(T.IH[:, 128 * h:128 * h + 128], float(h - 256)).then_inc(sem.m_ih, 1)
    v.wait_ge(sem.i_il, 1)
    v.tensor_scalar(T.IL[:, 128:256], T.IL[:, 0:128], 128.0, None, op.add).then_inc(sem.v_il1, 1)
    v.wait_ge(sem.v_il1, 1)
    v.tensor_scalar(T.IL[:, 256:512], T.IL[:, 0:256], 256.0, None, op.add).then_inc(sem.v_il2, 1)
    v.wait_ge(sem.m_ih, 4)
    v.wait_ge(sem.v_c, 4)
    v.tensor_scalar(T.IH[:], T.IH[:], cA, cB, op.mult, op.add).then_inc(sem.v_ih, 1)
    v.wait_ge(sem.v_il2, 1)
    v.tensor_scalar(T.IL[:], T.IL[:], cA, cB, op.mult, op.add).then_inc(sem.v_il, 1)
    v.wait_ge(sem.v_ih, 1)
    v.wait_ge(sem.v_il, 1)


def bank(T, n, h):
    return T.psA[:, 512 * h:512 * h + 512] if n == "H" else T.psC[:, 512 * (h % 3):512 * (h % 3) + 512]


def factors(g, T, end, n):
    op, sem, v, t = AluOpType, T.sem, g.vector, g.tensor
    hilo, hl, LH, RL = T["hilo" + n], T["hl" + n], T["LH" + n], T["RL" + n]
    v.tensor_scalar(hilo[:, 0:1], end, 9, None, op.arith_shift_right).then_inc(sem["hi" + n], 1)
    v.tensor_scalar(hilo[:, 1:2], end, 511, None, op.bitwise_and).then_inc(sem["hi" + n], 1)
    v.wait_ge(sem["hi" + n], 2)
    v.tensor_scalar(hl[:], hilo[:], T.cc[:, 0:1], T.cc[:, 2:3], op.mult, op.add).then_inc(sem["hl" + n], 1)
    v.wait_ge(sem["hl" + n], 1)
    v.tensor_scalar(LH[:], T.IH[:], hl[:, 0:1], -M, op.is_equal, op.mult).then_inc(sem["lr" + n], 1)
    v.tensor_scalar(RL[:], T.IL[:], hl[:, 1:2], T.cc[:, 3:4], op.is_equal, op.mult).then_inc(sem["lr" + n], 1)
    t.wait_ge(sem["lr" + n], 2)
    for h in range(4):
        if n == "O" and h == 3:
            t.wait_ge(sem.fO0, 1)
        t.matmul(bank(T, n, h), LH[:, 128 * h:128 * h + 128], RL[:], True, True).then_inc(sem["ps%s%d" % (n, h)], 1)


def copy_caps(g, T, F, n):
    sem, v, s = T.sem, g.vector, g.scalar
    for h in range(4):
        e = v if n == "H" and h % 2 else s
        e.wait_ge(sem["ps%s%d" % (n, h)], 1)
        out, src = F[:, 512 * h:512 * h + 512], bank(T, n, h)
        (s.activation(out, src, ActivationFunctionType.Copy) if e is s else v.tensor_copy(out, src)
         ).then_inc(sem["f%s%d" % (n, h)], 1)


def unpack(g, T, ent, end, before, waits):
    op, sem, v, t = AluOpType, T.sem, g.vector, g.tensor
    for name, n in waits:
        v.wait_ge(sem[name], n)
    v.tensor_copy(T.ef[:, 0:1], end).then_inc(sem.efU, 1)
    v.tensor_tensor(T.ef[:, 1:2], end, before, op.not_equal).then_inc(sem.efU, 1)
    v.wait_ge(sem.v_MK, 1)
    a, n = 128, 1
    if ent is not None:
        a, n = 0, 2
        v.wait_ge(sem.v_rep, 1)
        v.tensor_tensor(T.Z[:, 0:128], ent.indirect(T.rep[:]), T.MK[:, 0:128], op.mult).then_inc(sem.ZU, 1)
    v.wait_ge(sem.efU, 2)
    v.tensor_scalar(T.Z[:, 128:136], T.MK[:, 128:136], T.ef[:, 0:1], T.ef[:, 1:2], op.mult, op.mult).then_inc(sem.ZU, 1)
    t.wait_ge(sem.v_SEL, 1)
    t.wait_ge(sem.ZU, n)
    t.matmul(T.psB[:, a:136], T.SEL[:], T.Z[:, a:136], True, True).then_inc(sem.unU, 1)


def offsets(g, T, rank, out, done):
    op = AluOpType
    g.vector.tensor_scalar(out, T.psB[:, 0:128], float(PAD - rank * COLS), float(PAD + COLS), op.add, op.min).then_inc(done, 1)


def helper_program(g, core, main, q, T, topo):
    op, sem, v = AluOpType, T.sem, g.vector
    i, c = neighbours(main, T, topo)
    sent = []

    def send(dst, out, src, rsem):
        rid, pid = topo.addr(dst, core)
        mask = topo.mask(core, dst)
        g.remote_dma(out_ap=out, in_ap=src, remote_sem=rsem, local_sem=sem.loc, pid=pid, routing_id=rid, dma_engine_mask=mask)
        sent.append(len(engines(mask)))

    def send_caps(p, F, n):
        for k in range(2):
            g.wait_ge(sem["f%s%d" % (n, 2 * k)], 1)
            g.wait_ge(sem["f%s%d" % (n, 2 * k + 1)], 1)
            a = 1024 * k
            send(main, T["F" + p][:, a:a + 1024], F[:, a:a + 1024], sem["r_F%s%d" % (p, k)])

    g.iota(T.pcol[:], [[0, 8]], 0, 1).then_inc(sem.i_p, 1)
    g.iota(T.IL[:, 0:128], [[1, 128]], -256, 0, allow_small_or_imprecise_dtypes=True).then_inc(sem.i_il, 1)
    if q == "D":
        cap_constants(g, T)
        unpack_constants(g, T, False)
    else:
        unpack_constants(g, T, True)
        cap_constants(g, T)
    if q in AWAY:
        v.memset(T.SH[:, 0:1], 0.0).then_inc(sem.m_sH, 1)
    if q == HOME["O"]:
        v.wait_ge(sem.r_E, len(engines(list_masks(main, T, topo)["O"])))
        factors(g, T, T.E[:], "O")
        copy_caps(g, T, T.FO, "O")
        send_caps("O", T.FO, "O")

    if q == "D":
        end, before = T.EH[:, 0:1], T.EH[:, 1:2]
        unpack(g, T, None, end, before, [("r_XH", len(engines(topo.mask(helpers_of(i, T, topo)["C"], core))))])
    else:
        end, before = T.XH[:, 16:17], T.XH[:, 17:18]
        nx = len(engines(list_masks(c if q == "C" else i, T, topo)[q]))
        if q == "C":
            g.wait_ge(sem.r_XH, nx)
            send(helpers_of(i, T, topo)["D"], T.EH[:], T.XH[:, 16:18], sem.r_XH)
        unpack(g, T, T.XH[:, 0:16], end, before, [("r_XH", nx)])
        v.wait_ge(sem.unU, 1)
        if q == "C":
            offsets(g, T, T.rank_of(i), T.offH[:], sem.offH)
            offsets(g, T, T.rank_of(main), T.offC[:], sem.offC)
            g.wait_ge(sem.offH, 1)
            send(i, T.offD[:], T.offH[:], sem.r_offD)
            g.wait_ge(sem.offC, 1)
            send(main, T.offC[:], T.offC[:], sem.r_offC)
        else:
            offsets(g, T, T.rank_of(main), T.offI[:, 0:128], sem.offI)
            v.tensor_copy(T.offI[:, 128:136], T.psB[:, 128:136]).then_inc(sem.offI, 1)
            g.wait_ge(sem.offI, 2)
            send(main, T.offI[:], T.offI[:], sem.r_offI)
    factors(g, T, end, "H")
    if q in AWAY:
        if q == "D":
            v.wait_ge(sem.unU, 1)
        v.tensor_copy(T.pkH[:], T.psB[:, 128:136]).then_inc(sem.pkH, 1)
    copy_caps(g, T, T.FH, "H")
    if q not in AWAY:
        send_caps(q, T.FH, "H")
        g.wait_ge(sem.loc, sum(sent))
        return

    ng = len(engines(topo.mask(main, core)))
    for k, (a, b) in enumerate(PIECES):
        for h in range(a // 512, b // 512):
            v.wait_ge(sem["fH%d" % h], 1)
        v.wait_ge(sem["r_G%d" % k], ng)
        if k:
            v.wait_ge(sem["sH%d" % (k - 1)], 1)
        v.tensor_tensor_scan(T.SH[:, a + 1:b + 1], T.FH[:, a:b], T.GH[:, a:b], -M if a == 0 else T.SH[:, a:a + 1], op.min, op.max
                             ).then_inc(sem["sH%d" % k], 1)
    v.wait_ge(sem.m_sH, 1)
    v.wait_ge(sem.pkH, 1)
    v.wait_ge(sem["sH%d" % (len(PIECES) - 1)], 1)
    v.tensor_copy(T.PH[:], T.SH[:, 0:LEN + 1].indirect(T.pkH[:])).then_inc(sem.v_PH, 1)
    if q == "D":
        g.wait_ge(sem.v_PH, 1)
        send(helpers_of(i, T, topo)["C"], T.LD[:], T.PH[:], sem.r_LD)
    else:
        v.wait_ge(sem.v_PH, 1)
        v.wait_ge(sem.r_LD, len(engines(topo.mask(helpers_of(i, T, topo)["D"], core))))
        v.tensor_tensor(T.QH[:], T.PH[:], T.LD[:], op.max).then_inc(sem.v_QH, 1)
        g.wait_ge(sem.v_QH, 1)
        send(c, T.LC[:], T.QH[:], sem.r_LC)
    g.wait_ge(sem.loc, sum(sent))


def rank_program(g, core, T, topo):
    for r in T.cores:
        for q, h in helpers_of(r, T, topo).items():
            if core == h:
                helper_program(g, core, r, q, T, topo)
    if T.rank_of(core) is None:
        return
    op, fn, sem = AluOpType, ActivationFunctionType, T.sem
    v, s, y = g.vector, g.scalar, g.sync
    i, c = neighbours(core, T, topo)
    H, Hi, Hc = helpers_of(core, T, topo), helpers_of(i, T, topo), helpers_of(c, T, topo)
    masks = list_masks(core, T, topo)
    nf = {q: len(engines(topo.mask(H[HOME[q]], core))) for q in HOME}
    ready = {"O": ("offO", 2)}
    for q, h in (("C", H["C"]), ("I", H["I"]), ("D", Hi["C"])):
        ready[q] = ("r_off" + q, len(engines(topo.mask(h, core))))
    sent = []

    def send(dst, mask, out, src, rsem):
        rid, pid = topo.addr(dst, core)
        g.remote_dma(out_ap=out, in_ap=src, remote_sem=rsem, local_sem=sem.loc, pid=pid, routing_id=rid, dma_engine_mask=mask)
        sent.append(len(engines(mask)))

    y.dma_start(T.XO[:, 0:16], T.idx[:]).then_inc(sem.d_idx, 16)
    v.memset(T.XO[0:1, 16:18], 0).then_inc(sem.m_x, 1)
    y.wait_ge(sem.m_x, 1)
    y.dma_start(T.XO[1:8, 17:18], T.end[15:16, 0:7]).then_inc(sem.d_end, 16)
    s.wait_ge(sem.m_x, 1)
    s.dma_start(T.XO[:, 16:17], T.end[:]).then_inc(sem.d_end, 16)
    s.dma_start(T.XO[8:128, 17:18], T.end[0:15, :]).then_inc(sem.d_end, 16)
    a = 0
    for n, w in enumerate(TABS):
        if n == 1:
            y.wait_ge(sem.lx, len(engines(masks["C"] | masks["I"])))
        (y if n else s).dma_start(T.win[:, PAD + a:PAD + a + w], T.tab[:, a:a + w]).then_inc(sem["d_tab%d" % n], 16)
        a += w

    v.memset(T.win[:, 0:PAD], -M).then_inc(sem.m_win, 1)
    v.memset(T.win[:, PAD + COLS:PAD + COLS + PAD], -M).then_inc(sem.m_win, 1)
    g.iota(T.pcol[:], [[0, 8]], 0, 1).then_inc(sem.i_p, 1)
    for q in "OI":
        v.memset(T["S" + q][:, 0:1], 0.0).then_inc(sem["m_s" + q], 1)
    unpack_constants(g, T, True)
    unpack(g, T, T.XO[:, 0:16], T.XO[:, 16:17], T.XO[:, 17:18], [("m_x", 1), ("d_idx", 16), ("d_end", 48)])
    v.wait_ge(sem.unU, 1)
    offsets(g, T, T.rank_of(core), T.offO[:, 0:128], sem.offO)
    v.tensor_copy(T.offO[:, 128:136], T.psB[:, 128:136]).then_inc(sem.offO, 1)

    scans, gathers = {}, {}
    for st in S_ORDER + V_ORDER:
        if st[0] == "scan":
            scans.setdefault(st[1], []).append((st[2], st[3]))
        if st[0] == "g":
            gathers.setdefault(st[1], []).append((st[2], st[3]))
    waited = {}

    def wait(e, eng, name, n):
        if (eng, name) not in waited:
            waited[eng, name] = 1
            e.wait_ge(sem[name], n)

    def gath(e, eng, q, a, b):
        for k in range(len(TABS)):
            wait(e, eng, "d_tab%d" % k, 16)
        wait(e, eng, "m_win", 2)
        wait(e, eng, *ready[q])
        src, out = T.win[:].indirect(T["off" + q][:, a // 16:b // 16]), T["G" + q][:, a:b]
        ins = s.activation(out, src, fn.Copy) if eng == "s" else v.tensor_copy(out, src)
        ins.then_inc(sem["g%s%d" % (q, a)], 1)

    def scan(q, a, b):
        S = T["S" + q]
        for a2, b2 in gathers[q]:
            if a2 < b and b2 > a:
                wait(v, "v", "g%s%d" % (q, a2), 1)
        for k in range(a // 1024, (b + 1023) // 1024):
            wait(v, "v", "r_F%s%d" % (q, k), nf[q])
        for a2, b2 in scans[q]:
            if b2 == a:
                wait(v, "v", "s%s%d" % (q, a2), 1)
        v.tensor_tensor_scan(S[:, a + 1:b + 1], T["F" + q][:, a:b], T["G" + q][:, a:b], -M if a == 0 else S[:, a:a + 1],
                             op.min, op.max).then_inc(sem["s%s%d" % (q, a)], 1)

    def picked(q):
        wait(v, "v", "s%s%d" % (q, scans[q][-1][0]), 1)
        wait(v, "v", "m_s" + q, 1)
        wait(v, "v", *ready[q])
        return T["S" + q][:, 0:LEN + 1].indirect(T["off" + q][:, 128:136])

    for st in V_ORDER:
        what, q = st[0], st[1]
        if what == "g":
            gath(v, "v", q, st[2], st[3])
        elif what == "scan":
            scan(q, st[2], st[3])
        elif what == "pick":
            v.tensor_copy(T.PI[:], picked(q)).then_inc(sem.v_PI, 1)
        elif what == "acc":
            src = picked(q)
            v.wait_ge(sem.r_LI, len(engines(topo.mask(i, core))))
            v.tensor_tensor(T.acc[:], src, T.LI[:], op.max).then_inc(sem.v_acc, 1)
        else:
            v.wait_ge(sem.v_acc, 1)
            v.wait_ge(sem.r_LC, len(engines(topo.mask(Hc["C"], core))))
            v.tensor_tensor(T.Y[:], T.acc[:], T.LC[:], op.max).then_inc(sem.v_Y, 1)

    for st in S_ORDER:
        gath(s, "s", st[1], st[2], st[3])

    for name, n in (("d_idx", 16), ("d_end", 48), ("m_x", 1)):
        g.wait_ge(sem[name], n)
    calls = []
    for dst, mask in ((Hc["C"], masks["C"]), (Hi["I"], masks["I"])):
        rid, pid = topo.addr(dst, core)
        calls.append(RemoteDMATransfer(dst_ids=[DstId(rid=rid, pnc=pid)], dma_engine_mask=mask, remote_sem=sem.r_XH,
                                       srcs=[T.XO[:]], dsts=[T.XH[:]]))
    g.remote_dma_fused(calls, local_sem=sem.lx)
    send(H[HOME["O"]], masks["O"], T.E[:], T.XO[:, 16:17], sem.r_E)
    for q in "DC":
        done = set()
        for k, (a, b) in enumerate(PIECES):
            for a2, b2 in gathers[q]:
                if a2 < b and b2 > a and a2 not in done:
                    done.add(a2)
                    g.wait_ge(sem["g%s%d" % (q, a2)], 1)
            send(H[q], topo.mask(core, H[q]), T.GH[:, a:b], T["G" + q][:, a:b], sem["r_G%d" % k])
    g.wait_ge(sem.v_PI, 1)
    send(i, topo.mask(core, i), T.LI[:], T.PI[:], sem.r_LI)
    g.wait_ge(sem.loc, sum(sent))

    y.wait_ge(sem.v_Y, 1)
    y.dma_start(T.y[:], T.Y[:]).then_inc(sem.d_y, 16)
    y.wait_ge(sem.d_y, 16)
